import numpy as np
import ml_dtypes


def mxq(x, axis, fmt="e4m3"):
    dtype, down = {"e4m3": (ml_dtypes.float8_e4m3fn, 7), "e5m2": (ml_dtypes.float8_e5m2, 14)}[fmt]
    v = np.moveaxis(np.asarray(x, np.float32).astype(ml_dtypes.bfloat16).astype(np.float64), axis, -1)
    blocks = v.reshape(v.shape[:-1] + (-1, 32))
    amax = np.abs(blocks).max(-1, keepdims=True)
    byte = np.maximum(np.where(amax > 0, np.frexp(amax)[1] - 1 + 127, 0) - down, 1)
    scale = np.exp2(byte - 127.0)
    codes = (blocks / scale).astype(np.float32).astype(dtype).astype(np.float64)
    return np.moveaxis((codes * scale).reshape(v.shape), -1, axis)


WIDE = False


def mx_kscale(k):
    if not WIDE:
        return np.ones(k)
    levels = np.array([24, -24, 12, -12, 0])
    if k % 512:
        return np.exp2(np.random.permutation(np.resize(levels, k // 32))).repeat(32)
    a = np.empty((k // 512, 16))
    for p in range(k // 512):
        a[p, :8] = np.random.permutation(np.resize(levels, 8))
        for g in range(8):
            far = levels[np.abs(levels - a[p, g]) >= 10]
            a[p, g + 8] = far[np.random.randint(len(far))]
    return np.exp2(a.ravel()).repeat(32)


def f64(x):
    return np.asarray(x).astype(np.float64)


def striped(idx):
    return np.tile(idx.reshape(-1, 16).T, (8, 1)).astype(np.uint16)


def unstriped(offs):
    return offs[:16].T.reshape(-1).astype(np.int64)


E2M1 = np.array([0.0, 0.5, 1.0, 1.5, 2.0, 3.0, 4.0, 6.0, -0.0, -0.5, -1.0, -1.5, -2.0, -3.0, -4.0, -6.0])


def pack_weight(w, fmt):
    k, n = w.shape
    w = f64(np.asarray(w, np.float32).astype(ml_dtypes.bfloat16)).reshape(k // 32, 32, n)
    amax = np.abs(w).max(1)
    if fmt == "e4m3":
        byte = np.frexp(amax)[1] - 1 + 127 - 7
    else:
        mant, ex = np.frexp(amax / 6.0)
        byte = np.where(mant > 0.5, ex, ex - 1) + 127
    byte = np.clip(np.where(amax > 0, byte, 1), 1, 254)
    scaled = (w * np.exp2(127.0 - byte)[:, None, :]).reshape(k, n).astype(np.float32)
    by_word = np.ascontiguousarray(scaled.reshape(k // 512, 128, 4, n).transpose(0, 1, 3, 2))
    if fmt == "e4m3":
        words = by_word.astype(ml_dtypes.float8_e4m3fn).view(np.uint8)
    else:
        c = by_word.astype(ml_dtypes.float4_e2m1fn).view(np.uint8) & 0xF
        words = (c[..., 0::2] | (c[..., 1::2] << 4)).reshape(k // 512, 128, 2 * n)
    return np.ascontiguousarray(words), np.ascontiguousarray(byte.astype(np.uint8).reshape(k // 512, 16, n))


def unpack_weight(words, scales, fmt):
    g, _, n = scales.shape
    words = np.ascontiguousarray(words).reshape(g, 128, n, -1)
    if fmt == "e4m3":
        vals = words.view(ml_dtypes.float8_e4m3fn).astype(np.float64)
    else:
        nib = np.empty((g, 128, n, 4), np.uint8)
        nib[..., 0::2] = words & 0xF
        nib[..., 1::2] = words >> 4
        vals = E2M1[nib]
    vals = vals * np.repeat(np.exp2(scales.astype(np.float64) - 127.0), 8, axis=1)[..., None]
    return vals.transpose(0, 1, 3, 2).reshape(g * 512, n)


def pack_table4(v):
    words, scales = pack_weight(v, "e2m1")
    g, t = words.shape[0] // 2, v.shape[1]
    return np.ascontiguousarray(words.reshape(g, 2, 128, t, 2).transpose(0, 2, 3, 1, 4).reshape(g, 128, t, 4)), scales


def unpack_table4(words, scales):
    g, _, t, _ = words.shape
    return unpack_weight(words.reshape(g, 128, t, 2, 2).transpose(0, 3, 1, 2, 4).reshape(2 * g, 128, 2 * t), scales, "e2m1")


def planes(y):
    n, m = y.shape
    v = y.astype(np.float32).astype(ml_dtypes.bfloat16).astype(np.float64).reshape(n // 32, 32, m)
    top = np.abs(v).max(1)
    byte = np.clip(np.where(top > 0, np.frexp(top)[1] - 1 + 127 - 7, 1), 1, 254)
    codes = (v * np.exp2(127.0 - byte)[:, None, :]).reshape(n, m).astype(np.float32).astype(ml_dtypes.float8_e4m3fn).view(np.uint8)
    words = codes.reshape(n // 512, 128, 4, m).transpose(0, 1, 3, 2)
    return np.ascontiguousarray(words), np.ascontiguousarray(byte.astype(np.uint8).reshape(n // 512, 16, m))


K, R, N, T, J = 1024, 512, 512, 4096, 1024


def setup_inputs():
    n = np.random.standard_normal
    s = mx_kscale(K)[:, None]
    u = mx_kscale(R)[:, None]
    p_tab = pack_table4(n((K, T)) * s)
    p_wb = pack_weight(0.7 * n((K, N)) / np.sqrt(K) / s, "e4m3")
    p_dn = pack_weight(n((K, R)) / np.sqrt(K) / s * u.T, "e4m3")
    return {
        "tab_words": p_tab[0],
        "tab_scales": p_tab[1],
        "wb_words": p_wb[0],
        "wb_scales": p_wb[1],
        "dn_words": p_dn[0],
        "dn_scales": p_dn[1],
        "upw": (2.0 * n((R, N)) / np.sqrt(R) / u).astype(np.float32),
        "x0T": (n((N, T))).astype(np.float32),
        "b": (0.3 * n(N)).astype(np.float32),
        "offs": striped(np.random.permutation(T)[:J]),
    }


def reference(tab_words, tab_scales, wb_words, wb_scales, dn_words, dn_scales, upw, x0T, b, offs):
    idx = unstriped(offs)
    tab_ = unpack_table4(tab_words, tab_scales)[:, idx]
    wb_ = unpack_weight(wb_words, wb_scales, "e4m3")
    dn_ = unpack_weight(dn_words, dn_scales, "e4m3")
    hs = dn_.T @ tab_
    h = hs
    h_ = mxq(h, 0, "e4m3")
    upw_ = mxq(f64(upw), 0, "e4m3")
    y = wb_.T @ tab_ + upw_.T @ h_
    out_0 = f64(x0T)[:, idx] * (y + f64(b)[:, None]) + f64(x0T)[:, idx]
    return (out_0,) + planes(out_0)

@@ -1,0 +1,253 @@
+from contextlib import ExitStack
+
+import concourse.mybir as mybir
+
+K, R, N, T, J = 1024, 512, 512, 4096, 1024
+FLOPS = 2 * J * (K * R + K * N + R * N)
+
+F32 = mybir.dt.float32
+BF16 = mybir.dt.bfloat16
+I32 = mybir.dt.int32
+U32 = mybir.dt.uint32
+U16 = mybir.dt.uint16
+U8 = mybir.dt.uint8
+FP8X4 = mybir.dt.float8_e4m3fn_x4
+FP4X4 = mybir.dt.float4_e2m1fn_x4
+MULT = mybir.AluOpType.mult
+IDENTITY = mybir.ActivationFunctionType.Identity
+
+P = 128
+PACK = 4
+PASSES = K // (P * PACK)
+HALF = 512
+CHUNK = 128
+PIECES = (256, 256, 256, 128, 128)
+STORE_AFTER = {1: 0, 2: 512, 4: 768}
+
+
+def tile_list_xcross_noneP_kernel(
+    tc, tab_words, tab_scales, wb_words, wb_scales, dn_words, dn_scales, upw, x0T, b, offs, out_0, out_1, out_2
+):
+    nc = tc.nc
+    with ExitStack() as ctx:
+        keep = ctx.enter_context(tc.tile_pool(name="keep", bufs=1))
+        placed = ctx.enter_context(tc.tile_pool(name="placed", bufs=1))
+        h_psum = ctx.enter_context(tc.psum_pool(name="h_psum", bufs=4))
+        y_psum = ctx.enter_context(tc.psum_pool(name="y_psum", bufs=4))
+
+        def entries(j0, width):
+            return offsets[:, j0 // 16 : (j0 + width) // 16]
+
+        def load_words(words, pool, name, **place):
+            raw = pool.tile([P, PASSES, N], I32, name=name, **place)
+            nc.sync.dma_start(raw[:], words.rearrange("a p n i -> p a (n i)").bitcast(I32))
+            return raw
+
+        def cleared(pool, name, engine, **place):
+            raw = pool.tile([P, PASSES, N], U8, name=name, **place)
+            engine.memset(raw[:].bitcast(I32), 0)
+            return raw
+
+        def load_scale_rows(scales, raw, queue):
+            for quad in range(4):
+                queue.dma_start(
+                    raw[32 * quad : 32 * quad + 4].bitcast(I32),
+                    scales[:, 4 * quad : 4 * quad + 4, :].rearrange("a r n -> r a n").bitcast(I32),
+                )
+
+        def deal(raw, dtype, pool, name, **place):
+            dealt = pool.tile([P, PASSES, PACK, P], dtype, name=name, align_bytes=64, **place)
+            nc.vector.tensor_copy(
+                dealt[:].rearrange("p a t m -> p a m t"), raw[:].rearrange("p a (m t) -> p a m t", t=PACK)
+            )
+            return dealt
+
+        x0_rows = x0T.rearrange("(p t) c -> p t c", t=PACK)
+
+        def load_x0(t, pool, **place):
+            window = pool.tile([P, T], F32, name="x0_%d" % t, **place)
+            nc.sync.dma_start(window[:], x0_rows[:, t, :])
+            return window
+
+        offsets = keep.tile([P, J // 16], U16, name="offsets")
+        nc.sync.dma_start(offsets[:], offs)
+
+        scale_window = placed.tile([P, T], U8, name="scale_window", offset=2048)
+        nc.vector.memset(scale_window[:].bitcast(I32), 0)
+        dn_raw = load_words(dn_words, placed, "dn_raw", offset=36864)
+        for r in range(4):
+            nc.sync.dma_start(
+                scale_window[r:P:16, :].bitcast(I32),
+                tab_scales[:, r:16:4, :].rearrange("a q c -> q a c").bitcast(I32),
+            )
+        zeros = placed.tile([P, J // 4], I32, name="zeros", offset=20480)
+        nc.vector.memset(zeros[96:P, :], 0)
+        second_scales = keep.tile([P, J], U8, name="second_scales", align_bytes=64)
+        nc.vector.tensor_copy(second_scales[96:P, :].bitcast(I32), zeros[96:P, :])
+        word_window = placed.tile([P, T], I32, name="word_window", offset=20480)
+        nc.sync.dma_start(word_window[:], tab_words[0].rearrange("p t i -> p (t i)").bitcast(I32))
+        dn_scale_raw = cleared(placed, "dn_scale_raw", nc.vector, offset=65024)
+        load_scale_rows(dn_scales, dn_scale_raw, nc.sync)
+        wb_scale_raw = cleared(keep, "wb_scale_raw", nc.gpsimd)
+        load_scale_rows(wb_scales, wb_scale_raw, nc.gpsimd)
+        bias = keep.tile([P, PACK], F32, name="bias")
+        nc.gpsimd.dma_start(bias[:], b.rearrange("(p t) -> p t", t=PACK))
+
+
+        bias_one = keep.tile([P, PACK], F32, name="bias_one")
+        nc.scalar.activation(bias_one[:], bias[:], IDENTITY, bias=1.0)
+        dn_codes = deal(dn_raw, I32, keep, "dn_codes")
+        up_raw = placed.tile([P, PACK, N], F32, name="up_raw", offset=36864)
+        nc.sync.dma_start(up_raw[:], upw.rearrange("(p i) n -> p i n", i=PACK))
+
+        first_scales = keep.tile([P, J], U8, name="first_scales", align_bytes=64)
+        nc.vector.tensor_copy(first_scales[:], scale_window[:].indirect(offsets[:]))
+        nc.sync.dma_start(second_scales[0 : P - 16, :].bitcast(I32), first_scales[16:P, :].bitcast(I32))
+        wb_raw = load_words(wb_words, placed, "wb_raw", offset=0)
+        x0 = [load_x0(0, placed, offset=4096)]
+        v_scales = (first_scales, second_scales)
+
+        def gather_words(half):
+            picked = placed.tile([P, HALF], U32, name="picked%d" % half, offset=(45568, 65024)[half])
+            nc.vector.tensor_copy(picked[:], word_window[:].bitcast(U32).indirect(entries(half * HALF, HALF)))
+            parted = keep.tile([P, PASSES, HALF], U16, name="parted%d" % half, align_bytes=64)
+            nc.vector.tensor_copy(parted[:], picked[:].bitcast(U16).rearrange("p (j a) -> p a j", a=PASSES))
+            return parted
+
+        def first_stage(half):
+            rounded = keep.tile([P, HALF, PACK], BF16, name="h_rounded%d" % half, align_bytes=64)
+            for c0 in range(0, HALF, CHUNK):
+                bank = h_psum.tile([P, PACK, CHUNK], F32, name="h_bank")
+                for t in range(PACK):
+                    for a in range(PASSES):
+                        nc.tensor.matmul_mx(
+                            out=bank[:, t, :],
+                            lhsT=dn_codes[:, a, t, :].bitcast(FP8X4),
+                            lhsT_scale=dn_planes[:, a, t, :],
+                            rhs=v_codes[half][:, a, c0 : c0 + CHUNK].bitcast(FP4X4),
+                            rhs_scale=v_scales[a][:, half * HALF + c0 : half * HALF + c0 + CHUNK],
+                            start=(a == 0),
+                            stop=(a == PASSES - 1),
+                        )
+                nc.scalar.copy(rounded[:, c0 : c0 + CHUNK, :], bank[:].rearrange("p t j -> p j t"))
+            codes = keep.tile([P, HALF], I32, name="h_codes%d" % half, align_bytes=64)
+            scales = keep.tile([P, HALF], U8, name="h_scales%d" % half, align_bytes=64)
+            nc.vector.quantize_mx(
+                out=codes[:].bitcast(FP8X4), scales=scales[:], in_=rounded[:].rearrange("p j t -> p (j t)")
+            )
+            return codes, scales
+
+        v_codes = [gather_words(0)]
+        x0.append(load_x0(1, placed, offset=47104))
+        dn_planes = deal(dn_scale_raw, U8, placed, "dn_planes", offset=45056)
+        v_codes.append(gather_words(1))
+        x0.append(load_x0(2, placed, offset=20480))
+        x0.append(load_x0(3, placed, offset=66560))
+        wb_codes = deal(wb_raw, I32, keep, "wb_codes")
+        wb_planes = deal(wb_scale_raw, U8, placed, "wb_planes", offset=65536)
+
+        up_rounded = keep.tile([P, N * PACK], BF16, name="up_rounded", align_bytes=64)
+        up_dealt = up_rounded[:].rearrange("p (t m i) -> p m t i", t=PACK, i=PACK)
+        up_source = up_raw[:].rearrange("p i (m t) -> p m t i", t=PACK)
+        nc.scalar.copy(up_dealt, up_source)
+        up_codes = placed.tile([P, N], I32, name="up_codes", align_bytes=64, offset=63488)
+        up_planes = keep.tile([P, N], U8, name="up_planes", align_bytes=64)
+        nc.vector.quantize_mx(out=up_codes[:].bitcast(FP8X4), scales=up_planes[:], in_=up_rounded[:])
+
+        factor = {}
+
+        def second_stage(t, half):
+            h_codes, h_scales = h[half]
+            bank = y_psum.tile([P, HALF], F32, name="y_bank")
+            for a in range(PASSES):
+                nc.tensor.matmul_mx(
+                    out=bank[:],
+                    lhsT=wb_codes[:, a, t, :].bitcast(FP8X4),
+                    lhsT_scale=wb_planes[:, a, t, :],
+                    rhs=v_codes[half][:, a, :].bitcast(FP4X4),
+                    rhs_scale=v_scales[a][:, half * HALF : (half + 1) * HALF],
+                    start=(a == 0),
+                    stop=False,
+                )
+            nc.tensor.matmul_mx(
+                out=bank[:],
+                lhsT=up_codes[:, t * P : (t + 1) * P].bitcast(FP8X4),
+                lhsT_scale=up_planes[:, t * P : (t + 1) * P],
+                rhs=h_codes[:].bitcast(FP8X4),
+                rhs_scale=h_scales[:],
+                start=False,
+                stop=True,
+            )
+            factor[t, half] = keep.tile([P, HALF], F32, name="factor%d_%d" % (t, half))
+            nc.scalar.activation(factor[t, half][:], bank[:], IDENTITY, bias=bias_one[:, t : t + 1])
+
+        h = [first_stage(0)]
+        second_stage(0, 0)
+        second_stage(1, 0)
+        h.append(first_stage(1))
+        for t, half in ((2, 0), (0, 1), (1, 1), (2, 1), (3, 0), (3, 1)):
+            second_stage(t, half)
+
+        out_rows = out_0.rearrange("(p t) j -> p t j", t=PACK)
+        result = [keep.tile([P, 2, J], F32, name="result%d" % pair) for pair in range(2)]
+
+        def cross(t, j0, width):
+            half, c0 = divmod(j0, HALF)
+            nc.vector.tensor_tensor(
+                result[t // 2][:, t % 2, j0 : j0 + width],
+                x0[t][:].indirect(entries(j0, width)),
+                factor[t, half][:, c0 : c0 + width],
+                MULT,
+            )
+
+        starts = [sum(PIECES[:i]) for i in range(len(PIECES))]
+        rounded = [
+            keep.tile([P, width, PACK], BF16, name="out_rounded%d" % i, align_bytes=64)
+            for i, width in enumerate(PIECES)
+        ]
+
+        def round_pair(pair, i):
+            nc.scalar.copy(
+                rounded[i][:, :, 2 * pair : 2 * pair + 2],
+                result[pair][:, :, starts[i] : starts[i] + PIECES[i]].rearrange("p t j -> p j t"),
+            )
+
+        for half in range(J // HALF):
+            for t in range(2):
+                cross(t, half * HALF, HALF)
+        nc.sync.dma_start(out_rows[:, 0:2, :], result[0][:])
+        for i in range(len(PIECES)):
+            round_pair(0, i)
+        for half in range(J // HALF):
+            cross(2, half * HALF, HALF)
+        nc.sync.dma_start(out_rows[:, 2, :], result[1][:, 0, :])
+
+        out_codes = keep.tile([P, J], I32, name="out_codes", align_bytes=64)
+        out_scales = keep.tile([P, J], U8, name="out_scales", align_bytes=64)
+        code_rows = out_1[0].rearrange("p j i -> p (j i)").bitcast(I32)
+
+        def quantise(i):
+            cols = slice(starts[i], starts[i] + PIECES[i])
+            nc.vector.quantize_mx(
+                out=out_codes[:, cols].bitcast(FP8X4),
+                scales=out_scales[:, cols],
+                in_=rounded[i][:].rearrange("p j t -> p (j t)"),
+            )
+            if i in STORE_AFTER:
+                cols = slice(STORE_AFTER[i], starts[i] + PIECES[i])
+                nc.sync.dma_start(code_rows[:, cols], out_codes[:, cols])
+
+        for i in range(len(PIECES)):
+            cross(3, starts[i], PIECES[i])
+            if i in STORE_AFTER:
+                cols = slice(STORE_AFTER[i], starts[i] + PIECES[i])
+                nc.sync.dma_start(out_rows[:, 3, cols], result[1][:, 1, cols])
+            round_pair(1, i)
+            if i > 0:
+                quantise(i - 1)
+        quantise(len(PIECES) - 1)
+        for quad in range(4):
+            queue = nc.scalar if quad % 2 else nc.sync
+            queue.dma_start(
+                out_2[0, 4 * quad : 4 * quad + 4, :].bitcast(I32), out_scales[32 * quad : 32 * quad + 4, :].bitcast(I32)
+            )

@@ -57,9 +57,12 @@ def tile_list_xcross_noneP_kernel(
 
         def deal(raw, dtype, pool, name, **place):
             dealt = pool.tile([P, PASSES, PACK, P], dtype, name=name, align_bytes=64, **place)
-            nc.vector.tensor_copy(
-                dealt[:].rearrange("p a t m -> p a m t"), raw[:].rearrange("p a (m t) -> p a m t", t=PACK)
-            )
+            if dtype == U8:
+                nc.vector.tensor_copy(dealt[:], raw[:].rearrange("p a (m t) -> p a t m", t=PACK))
+            else:
+                nc.vector.tensor_copy(
+                    dealt[:].rearrange("p a t m -> p a m t"), raw[:].rearrange("p a (m t) -> p a m t", t=PACK)
+                )
             return dealt
 
         x0_rows = x0T.rearrange("(p t) c -> p t c", t=PACK)

@@ -19,6 +19,7 @@ IDENTITY = mybir.ActivationFunctionType.Identity
 P = 128
 PACK = 4
 PASSES = K // (P * PACK)
+ROW0 = 96
 HALF = 512
 CHUNK = 128
 PIECES = (256, 256, 256, 128, 128)
@@ -38,77 +39,64 @@ def tile_list_xcross_noneP_kernel(
         def entries(j0, width):
             return offsets[:, j0 // 16 : (j0 + width) // 16]
 
-        def load_words(words, pool, name, **place):
-            raw = pool.tile([P, PASSES, N], I32, name=name, **place)
+        def load_words(words, name, offset):
+            raw = placed.tile([P, PASSES, N], I32, name=name, offset=offset)
             nc.sync.dma_start(raw[:], words.rearrange("a p n i -> p a (n i)").bitcast(I32))
             return raw
 
-        def cleared(pool, name, engine, **place):
-            raw = pool.tile([P, PASSES, N], U8, name=name, **place)
-            engine.memset(raw[:].bitcast(I32), 0)
-            return raw
-
-        def load_scale_rows(scales, raw, queue):
-            for quad in range(4):
-                queue.dma_start(
-                    raw[32 * quad : 32 * quad + 4].bitcast(I32),
-                    scales[:, 4 * quad : 4 * quad + 4, :].rearrange("a r n -> r a n").bitcast(I32),
-                )
-
-        def deal(raw, dtype, pool, name, **place):
-            dealt = pool.tile([P, PASSES, PACK, P], dtype, name=name, align_bytes=64, **place)
-            if dtype == U8:
-                nc.vector.tensor_copy(dealt[:], raw[:].rearrange("p a (m t) -> p a t m", t=PACK))
-            else:
-                nc.vector.tensor_copy(
-                    dealt[:].rearrange("p a t m -> p a m t"), raw[:].rearrange("p a (m t) -> p a m t", t=PACK)
-                )
+        def deal_words(raw, name):
+            dealt = keep.tile([P, PASSES, PACK, P], I32, name=name, align_bytes=64)
+            nc.vector.tensor_copy(
+                dealt[:].rearrange("p a t m -> p a m t"), raw[:].rearrange("p a (m t) -> p a m t", t=PACK)
+            )
             return dealt
 
         x0_rows = x0T.rearrange("(p t) c -> p t c", t=PACK)
 
-        def load_x0(t, pool, **place):
-            window = pool.tile([P, T], F32, name="x0_%d" % t, **place)
+        def load_x0(t, offset):
+            window = placed.tile([P, T], F32, name="x0_%d" % t, offset=offset)
             nc.sync.dma_start(window[:], x0_rows[:, t, :])
             return window
 
         offsets = keep.tile([P, J // 16], U16, name="offsets")
         nc.sync.dma_start(offsets[:], offs)
 
-        scale_window = placed.tile([P, T], U8, name="scale_window", offset=2048)
-        nc.vector.memset(scale_window[:].bitcast(I32), 0)
-        dn_raw = load_words(dn_words, placed, "dn_raw", offset=36864)
-        for r in range(4):
-            nc.sync.dma_start(
-                scale_window[r:P:16, :].bitcast(I32),
-                tab_scales[:, r:16:4, :].rearrange("a q c -> q a c").bitcast(I32),
-            )
-        zeros = placed.tile([P, J // 4], I32, name="zeros", offset=20480)
-        nc.vector.memset(zeros[96:P, :], 0)
-        second_scales = keep.tile([P, J], U8, name="second_scales", align_bytes=64)
-        nc.vector.tensor_copy(second_scales[96:P, :].bitcast(I32), zeros[96:P, :])
+        scale_window = keep.tile([P, T], U8, name="scale_window")
+        weight_scales = keep.tile([P, 2, N], U8, name="weight_scales")
+        nc.sync.dma_start(scale_window[ROW0:P, :].bitcast(I32), tab_scales.rearrange("a q c -> q a c").bitcast(I32))
+        for w, scales in enumerate((dn_scales, wb_scales)):
+            nc.sync.dma_start(weight_scales[ROW0:P, w, :].bitcast(I32), scales.rearrange("a q n -> q a n").bitcast(I32))
         word_window = placed.tile([P, T], I32, name="word_window", offset=20480)
         nc.sync.dma_start(word_window[:], tab_words[0].rearrange("p t i -> p (t i)").bitcast(I32))
-        dn_scale_raw = cleared(placed, "dn_scale_raw", nc.vector, offset=65024)
-        load_scale_rows(dn_scales, dn_scale_raw, nc.sync)
-        wb_scale_raw = cleared(keep, "wb_scale_raw", nc.gpsimd)
-        load_scale_rows(wb_scales, wb_scale_raw, nc.gpsimd)
+        dn_raw = load_words(dn_words, "dn_raw", 62464)
+        up_raw = keep.tile([P, PACK, N], F32, name="up_raw")
+        nc.sync.dma_start(up_raw[:], upw.rearrange("(p i) n -> p i n", i=PACK))
         bias = keep.tile([P, PACK], F32, name="bias")
-        nc.gpsimd.dma_start(bias[:], b.rearrange("(p t) -> p t", t=PACK))
+        nc.sync.dma_start(bias[:], b.rearrange("(p t) -> p t", t=PACK))
 
+        nc.vector.memset(scale_window[0:ROW0, :].bitcast(I32), 0)
+        nc.vector.memset(weight_scales[0:ROW0].bitcast(I32), 0)
+        planes = keep.tile([P, PASSES, J + 2 * N], U8, name="planes", align_bytes=64)
+        nc.vector.memset(planes[:].bitcast(I32), 0)
 
         bias_one = keep.tile([P, PACK], F32, name="bias_one")
         nc.scalar.activation(bias_one[:], bias[:], IDENTITY, bias=1.0)
-        dn_codes = deal(dn_raw, I32, keep, "dn_codes")
-        up_raw = placed.tile([P, PACK, N], F32, name="up_raw", offset=36864)
-        nc.sync.dma_start(up_raw[:], upw.rearrange("(p i) n -> p i n", i=PACK))
 
-        first_scales = keep.tile([P, J], U8, name="first_scales", align_bytes=64)
-        nc.vector.tensor_copy(first_scales[:], scale_window[:].indirect(offsets[:]))
-        nc.sync.dma_start(second_scales[0 : P - 16, :].bitcast(I32), first_scales[16:P, :].bitcast(I32))
-        wb_raw = load_words(wb_words, placed, "wb_raw", offset=0)
-        x0 = [load_x0(0, placed, offset=4096)]
-        v_scales = (first_scales, second_scales)
+        picked_scales = placed.tile([P, J], U8, name="picked_scales", offset=3584)
+        nc.vector.tensor_copy(picked_scales[:], scale_window[:].indirect(offsets[:]))
+        scale_rows = keep.tile([P, J + 2 * N], U8, name="scale_rows")
+        nc.vector.tensor_copy(
+            scale_rows[:, J:].rearrange("p (w t m) -> p w t m", w=2, t=PACK),
+            weight_scales[:].rearrange("p w (m t) -> p w t m", t=PACK),
+        )
+        nc.vector.tensor_copy(scale_rows[:, 0:J].bitcast(I32), picked_scales[:].bitcast(I32))
+        for quad in range(4):
+            nc.sync.dma_start(
+                planes[32 * quad : 32 * quad + 4].bitcast(I32),
+                scale_rows[ROW0 + 8 * quad : ROW0 + 8 * quad + 8, :].bitcast(I32),
+            )
+        wb_raw = load_words(wb_words, "wb_raw", 0)
+        x0 = [load_x0(0, 4096)]
 
         def gather_words(half):
             picked = placed.tile([P, HALF], U32, name="picked%d" % half, offset=(45568, 65024)[half])
@@ -126,9 +114,9 @@ def tile_list_xcross_noneP_kernel(
                         nc.tensor.matmul_mx(
                             out=bank[:, t, :],
                             lhsT=dn_codes[:, a, t, :].bitcast(FP8X4),
-                            lhsT_scale=dn_planes[:, a, t, :],
+                            lhsT_scale=planes[:, a, J + t * P : J + (t + 1) * P],
                             rhs=v_codes[half][:, a, c0 : c0 + CHUNK].bitcast(FP4X4),
-                            rhs_scale=v_scales[a][:, half * HALF + c0 : half * HALF + c0 + CHUNK],
+                            rhs_scale=planes[:, a, half * HALF + c0 : half * HALF + c0 + CHUNK],
                             start=(a == 0),
                             stop=(a == PASSES - 1),
                         )
@@ -141,13 +129,12 @@ def tile_list_xcross_noneP_kernel(
             return codes, scales
 
         v_codes = [gather_words(0)]
-        x0.append(load_x0(1, placed, offset=47104))
-        dn_planes = deal(dn_scale_raw, U8, placed, "dn_planes", offset=45056)
+        x0.append(load_x0(1, 45568))
+        dn_codes = deal_words(dn_raw, "dn_codes")
         v_codes.append(gather_words(1))
-        x0.append(load_x0(2, placed, offset=20480))
-        x0.append(load_x0(3, placed, offset=66560))
-        wb_codes = deal(wb_raw, I32, keep, "wb_codes")
-        wb_planes = deal(wb_scale_raw, U8, placed, "wb_planes", offset=65536)
+        x0.append(load_x0(2, 20480))
+        x0.append(load_x0(3, 66560))
+        wb_codes = deal_words(wb_raw, "wb_codes")
 
         up_rounded = keep.tile([P, N * PACK], BF16, name="up_rounded", align_bytes=64)
         up_dealt = up_rounded[:].rearrange("p (t m i) -> p m t i", t=PACK, i=PACK)
@@ -166,9 +153,9 @@ def tile_list_xcross_noneP_kernel(
                 nc.tensor.matmul_mx(
                     out=bank[:],
                     lhsT=wb_codes[:, a, t, :].bitcast(FP8X4),
-                    lhsT_scale=wb_planes[:, a, t, :],
+                    lhsT_scale=planes[:, a, J + N + t * P : J + N + (t + 1) * P],
                     rhs=v_codes[half][:, a, :].bitcast(FP4X4),
-                    rhs_scale=v_scales[a][:, half * HALF : (half + 1) * HALF],
+                    rhs_scale=planes[:, a, half * HALF : (half + 1) * HALF],
                     start=(a == 0),
                     stop=False,
                 )

@@ -14,6 +14,7 @@ U8 = mybir.dt.uint8
 FP8X4 = mybir.dt.float8_e4m3fn_x4
 FP4X4 = mybir.dt.float4_e2m1fn_x4
 MULT = mybir.AluOpType.mult
+ADD = mybir.AluOpType.add
 IDENTITY = mybir.ActivationFunctionType.Identity
 
 P = 128
@@ -22,8 +23,8 @@ PASSES = K // (P * PACK)
 ROW0 = 96
 HALF = 512
 CHUNK = 128
-PIECES = (256, 256, 256, 128, 128)
-STORE_AFTER = {1: 0, 2: 512, 4: 768}
+PIECES = (256, 256, 256, 256)
+STORE_AFTER = {1: 0, 2: 512, 3: 768}
 
 
 def tile_list_xcross_noneP_kernel(
@@ -33,8 +34,7 @@ def tile_list_xcross_noneP_kernel(
     with ExitStack() as ctx:
         keep = ctx.enter_context(tc.tile_pool(name="keep", bufs=1))
         placed = ctx.enter_context(tc.tile_pool(name="placed", bufs=1))
-        h_psum = ctx.enter_context(tc.psum_pool(name="h_psum", bufs=4))
-        y_psum = ctx.enter_context(tc.psum_pool(name="y_psum", bufs=4))
+        psum = ctx.enter_context(tc.psum_pool(name="psum", bufs=8))
 
         def entries(j0, width):
             return offsets[:, j0 // 16 : (j0 + width) // 16]
@@ -108,7 +108,7 @@ def tile_list_xcross_noneP_kernel(
         def first_stage(half):
             rounded = keep.tile([P, HALF, PACK], BF16, name="h_rounded%d" % half, align_bytes=64)
             for c0 in range(0, HALF, CHUNK):
-                bank = h_psum.tile([P, PACK, CHUNK], F32, name="h_bank")
+                bank = psum.tile([P, PACK, CHUNK], F32, name="h_bank", tag="bank")
                 for t in range(PACK):
                     for a in range(PASSES):
                         nc.tensor.matmul_mx(
@@ -144,11 +144,9 @@ def tile_list_xcross_noneP_kernel(
         up_planes = keep.tile([P, N], U8, name="up_planes", align_bytes=64)
         nc.vector.quantize_mx(out=up_codes[:].bitcast(FP8X4), scales=up_planes[:], in_=up_rounded[:])
 
-        factor = {}
-
         def second_stage(t, half):
             h_codes, h_scales = h[half]
-            bank = y_psum.tile([P, HALF], F32, name="y_bank")
+            bank = psum.tile([P, HALF], F32, name="y_bank", tag="bank")
             for a in range(PASSES):
                 nc.tensor.matmul_mx(
                     out=bank[:],
@@ -168,49 +166,57 @@ def tile_list_xcross_noneP_kernel(
                 start=False,
                 stop=True,
             )
-            factor[t, half] = keep.tile([P, HALF], F32, name="factor%d_%d" % (t, half))
-            nc.scalar.activation(factor[t, half][:], bank[:], IDENTITY, bias=bias_one[:, t : t + 1])
-
-        h = [first_stage(0)]
-        second_stage(0, 0)
-        second_stage(1, 0)
-        h.append(first_stage(1))
-        for t, half in ((2, 0), (0, 1), (1, 1), (2, 1), (3, 0), (3, 1)):
-            second_stage(t, half)
+            return bank
 
         out_rows = out_0.rearrange("(p t) j -> p t j", t=PACK)
-        result = [keep.tile([P, 2, J], F32, name="result%d" % pair) for pair in range(2)]
-
-        def cross(t, j0, width):
-            half, c0 = divmod(j0, HALF)
-            nc.vector.tensor_tensor(
-                result[t // 2][:, t % 2, j0 : j0 + width],
-                x0[t][:].indirect(entries(j0, width)),
-                factor[t, half][:, c0 : c0 + width],
-                MULT,
-            )
-
+        low = [keep.tile([P, 2, HALF], F32, name="low%d" % half) for half in range(2)]
+        high = keep.tile([P, 2, J], F32, name="high")
         starts = [sum(PIECES[:i]) for i in range(len(PIECES))]
         rounded = [
             keep.tile([P, width, PACK], BF16, name="out_rounded%d" % i, align_bytes=64)
             for i, width in enumerate(PIECES)
         ]
 
-        def round_pair(pair, i):
-            nc.scalar.copy(
-                rounded[i][:, :, 2 * pair : 2 * pair + 2],
-                result[pair][:, :, starts[i] : starts[i] + PIECES[i]].rearrange("p t j -> p j t"),
-            )
+        def gather_x0(t):
+            picked = keep.tile([P, J], F32, name="x0_picked%d" % t)
+            nc.vector.tensor_copy(picked[:], x0[t][:].indirect(offsets[:]))
+            return picked
 
+        def cross(t, half, bank):
+            cols = slice(half * HALF, (half + 1) * HALF)
+            result = low[half][:, t, :] if t < 2 else high[:, 0, cols]
+            nc.vector.scalar_tensor_tensor(result, bank[:], bias_one[:, t : t + 1], x0_picked[t][:, cols], ADD, MULT)
+
+        def finish_low(half):
+            nc.sync.dma_start(out_rows[:, 0:2, half * HALF : (half + 1) * HALF], low[half][:])
+            for i in range(len(PIECES)):
+                if starts[i] // HALF == half:
+                    c0 = starts[i] - half * HALF
+                    nc.scalar.copy(
+                        rounded[i][:, :, 0:2], low[half][:, :, c0 : c0 + PIECES[i]].rearrange("p t j -> p j t")
+                    )
+
+        h = [first_stage(0)]
+        y = {(0, 0): second_stage(0, 0), (1, 0): second_stage(1, 0)}
+        h.append(first_stage(1))
+        x0_picked = [gather_x0(0)]
+        cross(0, 0, y[0, 0])
+        y[2, 0] = second_stage(2, 0)
+        cross(0, 1, second_stage(0, 1))
+        x0_picked.append(gather_x0(1))
+        cross(1, 0, y[1, 0])
+        finish_low(0)
+        cross(1, 1, second_stage(1, 1))
+        finish_low(1)
+        x0_picked.append(gather_x0(2))
+        cross(2, 0, y[2, 0])
+        cross(2, 1, second_stage(2, 1))
+        nc.sync.dma_start(out_rows[:, 2, :], high[:, 0, :])
+        factor = keep.tile([P, J], F32, name="factor")
         for half in range(J // HALF):
-            for t in range(2):
-                cross(t, half * HALF, HALF)
-        nc.sync.dma_start(out_rows[:, 0:2, :], result[0][:])
-        for i in range(len(PIECES)):
-            round_pair(0, i)
-        for half in range(J // HALF):
-            cross(2, half * HALF, HALF)
-        nc.sync.dma_start(out_rows[:, 2, :], result[1][:, 0, :])
+            nc.scalar.activation(
+                factor[:, half * HALF : (half + 1) * HALF], second_stage(3, half)[:], IDENTITY, bias=bias_one[:, 3:4]
+            )
 
         out_codes = keep.tile([P, J], I32, name="out_codes", align_bytes=64)
         out_scales = keep.tile([P, J], U8, name="out_scales", align_bytes=64)
@@ -228,11 +234,15 @@ def tile_list_xcross_noneP_kernel(
                 nc.sync.dma_start(code_rows[:, cols], out_codes[:, cols])
 
         for i in range(len(PIECES)):
-            cross(3, starts[i], PIECES[i])
+            piece = slice(starts[i], starts[i] + PIECES[i])
+            nc.vector.tensor_tensor(
+                high[:, 1, piece], x0[3][:].indirect(entries(starts[i], PIECES[i])), factor[:, piece], MULT
+            )
             if i in STORE_AFTER:
                 cols = slice(STORE_AFTER[i], starts[i] + PIECES[i])
-                nc.sync.dma_start(out_rows[:, 3, cols], result[1][:, 1, cols])
-            round_pair(1, i)
+                nc.sync.dma_start(out_rows[:, 3, cols], high[:, 1, cols])
+            copy = nc.vector.tensor_copy if i == len(PIECES) - 1 else nc.scalar.copy
+            copy(rounded[i][:, :, 2:4], high[:, :, piece].rearrange("p t j -> p j t"))
             if i > 0:
                 quantise(i - 1)
         quantise(len(PIECES) - 1)

@@ -63,43 +63,43 @@ def tile_list_xcross_noneP_kernel(
 
         scale_window = keep.tile([P, T], U8, name="scale_window")
         weight_scales = keep.tile([P, 2, N], U8, name="weight_scales")
-        nc.sync.dma_start(scale_window[ROW0:P, :].bitcast(I32), tab_scales.rearrange("a q c -> q a c").bitcast(I32))
         for w, scales in enumerate((dn_scales, wb_scales)):
             nc.sync.dma_start(weight_scales[ROW0:P, w, :].bitcast(I32), scales.rearrange("a q n -> q a n").bitcast(I32))
-        word_window = placed.tile([P, T], I32, name="word_window", offset=20480)
+        nc.sync.dma_start(scale_window[ROW0:P, :].bitcast(I32), tab_scales.rearrange("a q c -> q a c").bitcast(I32))
+        word_window = placed.tile([P, T], I32, name="word_window", offset=24576)
         nc.sync.dma_start(word_window[:], tab_words[0].rearrange("p t i -> p (t i)").bitcast(I32))
-        dn_raw = load_words(dn_words, "dn_raw", 62464)
-        up_raw = keep.tile([P, PACK, N], F32, name="up_raw")
-        nc.sync.dma_start(up_raw[:], upw.rearrange("(p i) n -> p i n", i=PACK))
+        dn_raw = load_words(dn_words, "dn_raw", 57344)
+        wb_raw = load_words(wb_words, "wb_raw", 77824)
         bias = keep.tile([P, PACK], F32, name="bias")
         nc.sync.dma_start(bias[:], b.rearrange("(p t) -> p t", t=PACK))
 
-        nc.vector.memset(scale_window[0:ROW0, :].bitcast(I32), 0)
         nc.vector.memset(weight_scales[0:ROW0].bitcast(I32), 0)
+        nc.vector.memset(scale_window[0:ROW0, :].bitcast(I32), 0)
         planes = keep.tile([P, PASSES, J + 2 * N], U8, name="planes", align_bytes=64)
         nc.vector.memset(planes[:].bitcast(I32), 0)
 
         bias_one = keep.tile([P, PACK], F32, name="bias_one")
         nc.scalar.activation(bias_one[:], bias[:], IDENTITY, bias=1.0)
 
-        picked_scales = placed.tile([P, J], U8, name="picked_scales", offset=3584)
-        nc.vector.tensor_copy(picked_scales[:], scale_window[:].indirect(offsets[:]))
         scale_rows = keep.tile([P, J + 2 * N], U8, name="scale_rows")
         nc.vector.tensor_copy(
             scale_rows[:, J:].rearrange("p (w t m) -> p w t m", w=2, t=PACK),
             weight_scales[:].rearrange("p w (m t) -> p w t m", t=PACK),
         )
+        picked_scales = placed.tile([P, J], U8, name="picked_scales", offset=7680)
+        nc.vector.tensor_copy(picked_scales[:], scale_window[:].indirect(offsets[:]))
         nc.vector.tensor_copy(scale_rows[:, 0:J].bitcast(I32), picked_scales[:].bitcast(I32))
-        for quad in range(4):
+        for quad in (0, 2, 1, 3):
             nc.sync.dma_start(
                 planes[32 * quad : 32 * quad + 4].bitcast(I32),
                 scale_rows[ROW0 + 8 * quad : ROW0 + 8 * quad + 8, :].bitcast(I32),
             )
-        wb_raw = load_words(wb_words, "wb_raw", 0)
-        x0 = [load_x0(0, 4096)]
+        up_raw = placed.tile([P, PACK, N], F32, name="up_raw", offset=0)
+        nc.sync.dma_start(up_raw[:], upw.rearrange("(p i) n -> p i n", i=PACK))
+        x0 = [load_x0(0, 8192)]
 
         def gather_words(half):
-            picked = placed.tile([P, HALF], U32, name="picked%d" % half, offset=(45568, 65024)[half])
+            picked = placed.tile([P, HALF], U32, name="picked%d" % half, offset=(40960, 60416)[half])
             nc.vector.tensor_copy(picked[:], word_window[:].bitcast(U32).indirect(entries(half * HALF, HALF)))
             parted = keep.tile([P, PASSES, HALF], U16, name="parted%d" % half, align_bytes=64)
             nc.vector.tensor_copy(parted[:], picked[:].bitcast(U16).rearrange("p (j a) -> p a j", a=PASSES))
@@ -129,18 +129,18 @@ def tile_list_xcross_noneP_kernel(
             return codes, scales
 
         v_codes = [gather_words(0)]
-        x0.append(load_x0(1, 45568))
+        x0.append(load_x0(1, 40960))
         dn_codes = deal_words(dn_raw, "dn_codes")
         v_codes.append(gather_words(1))
-        x0.append(load_x0(2, 20480))
-        x0.append(load_x0(3, 66560))
+        x0.append(load_x0(2, 24576))
+        x0.append(load_x0(3, 61440))
         wb_codes = deal_words(wb_raw, "wb_codes")
 
         up_rounded = keep.tile([P, N * PACK], BF16, name="up_rounded", align_bytes=64)
         up_dealt = up_rounded[:].rearrange("p (t m i) -> p m t i", t=PACK, i=PACK)
         up_source = up_raw[:].rearrange("p i (m t) -> p m t i", t=PACK)
-        nc.scalar.copy(up_dealt, up_source)
-        up_codes = placed.tile([P, N], I32, name="up_codes", align_bytes=64, offset=63488)
+        nc.vector.tensor_copy(up_dealt, up_source)
+        up_codes = keep.tile([P, N], I32, name="up_codes", align_bytes=64)
         up_planes = keep.tile([P, N], U8, name="up_planes", align_bytes=64)
         nc.vector.quantize_mx(out=up_codes[:].bitcast(FP8X4), scales=up_planes[:], in_=up_rounded[:])
 
@@ -169,7 +169,7 @@ def tile_list_xcross_noneP_kernel(
             return bank
 
         out_rows = out_0.rearrange("(p t) j -> p t j", t=PACK)
-        low = [keep.tile([P, 2, HALF], F32, name="low%d" % half) for half in range(2)]
+        low = keep.tile([P, 2, J], F32, name="low")
         high = keep.tile([P, 2, J], F32, name="high")
         starts = [sum(PIECES[:i]) for i in range(len(PIECES))]
         rounded = [
@@ -177,46 +177,32 @@ def tile_list_xcross_noneP_kernel(
             for i, width in enumerate(PIECES)
         ]
 
-        def gather_x0(t):
-            picked = keep.tile([P, J], F32, name="x0_picked%d" % t)
-            nc.vector.tensor_copy(picked[:], x0[t][:].indirect(offsets[:]))
-            return picked
+        h = [first_stage(half) for half in range(2)]
+        y = {(t, half): second_stage(t, half) for t, half in ((0, 0), (1, 0), (0, 1), (1, 1), (2, 0), (2, 1), (3, 0), (3, 1))}
 
-        def cross(t, half, bank):
+        def make_factor(t):
+            made = keep.tile([P, J], F32, name="factor%d" % t)
+            for half in range(2):
+                nc.scalar.activation(
+                    made[:, half * HALF : (half + 1) * HALF], y[t, half][:], IDENTITY, bias=bias_one[:, t : t + 1]
+                )
+            return made
+
+        x0_picked = keep.tile([P, J], F32, name="x0_picked")
+        nc.vector.tensor_copy(x0_picked[:], x0[0][:].indirect(offsets[:]))
+        for half in range(2):
             cols = slice(half * HALF, (half + 1) * HALF)
-            result = low[half][:, t, :] if t < 2 else high[:, 0, cols]
-            nc.vector.scalar_tensor_tensor(result, bank[:], bias_one[:, t : t + 1], x0_picked[t][:, cols], ADD, MULT)
-
-        def finish_low(half):
-            nc.sync.dma_start(out_rows[:, 0:2, half * HALF : (half + 1) * HALF], low[half][:])
-            for i in range(len(PIECES)):
-                if starts[i] // HALF == half:
-                    c0 = starts[i] - half * HALF
-                    nc.scalar.copy(
-                        rounded[i][:, :, 0:2], low[half][:, :, c0 : c0 + PIECES[i]].rearrange("p t j -> p j t")
-                    )
-
-        h = [first_stage(0)]
-        y = {(0, 0): second_stage(0, 0), (1, 0): second_stage(1, 0)}
-        h.append(first_stage(1))
-        x0_picked = [gather_x0(0)]
-        cross(0, 0, y[0, 0])
-        y[2, 0] = second_stage(2, 0)
-        cross(0, 1, second_stage(0, 1))
-        x0_picked.append(gather_x0(1))
-        cross(1, 0, y[1, 0])
-        finish_low(0)
-        cross(1, 1, second_stage(1, 1))
-        finish_low(1)
-        x0_picked.append(gather_x0(2))
-        cross(2, 0, y[2, 0])
-        cross(2, 1, second_stage(2, 1))
-        nc.sync.dma_start(out_rows[:, 2, :], high[:, 0, :])
-        factor = keep.tile([P, J], F32, name="factor")
-        for half in range(J // HALF):
-            nc.scalar.activation(
-                factor[:, half * HALF : (half + 1) * HALF], second_stage(3, half)[:], IDENTITY, bias=bias_one[:, 3:4]
+            nc.vector.scalar_tensor_tensor(low[:, 0, cols], y[0, half][:], bias_one[:, 0:1], x0_picked[:, cols], ADD, MULT)
+        factors = [make_factor(t) for t in (1, 2, 3)]
+        factor = factors[2]
+        nc.vector.tensor_tensor(low[:, 1, :], x0[1][:].indirect(offsets[:]), factors[0][:], MULT)
+        nc.sync.dma_start(out_rows[:, 0:2, :], low[:])
+        for i in range(len(PIECES)):
+            nc.scalar.copy(
+                rounded[i][:, :, 0:2], low[:, :, starts[i] : starts[i] + PIECES[i]].rearrange("p t j -> p j t")
             )
+        nc.vector.tensor_tensor(high[:, 0, :], x0[2][:].indirect(offsets[:]), factors[1][:], MULT)
+        nc.sync.dma_start(out_rows[:, 2, :], high[:, 0, :])
 
         out_codes = keep.tile([P, J], I32, name="out_codes", align_bytes=64)
         out_scales = keep.tile([P, J], U8, name="out_scales", align_bytes=64)

@@ -63,15 +63,15 @@ def tile_list_xcross_noneP_kernel(
 
         scale_window = keep.tile([P, T], U8, name="scale_window")
         weight_scales = keep.tile([P, 2, N], U8, name="weight_scales")
-        for w, scales in enumerate((dn_scales, wb_scales)):
-            nc.sync.dma_start(weight_scales[ROW0:P, w, :].bitcast(I32), scales.rearrange("a q n -> q a n").bitcast(I32))
+        nc.scalar.dma_start(weight_scales[ROW0:P, 0, :].bitcast(I32), dn_scales.rearrange("a q n -> q a n").bitcast(I32))
+        nc.scalar.dma_start(weight_scales[ROW0:P, 1, :].bitcast(I32), wb_scales.rearrange("a q n -> q a n").bitcast(I32))
         nc.sync.dma_start(scale_window[ROW0:P, :].bitcast(I32), tab_scales.rearrange("a q c -> q a c").bitcast(I32))
         word_window = placed.tile([P, T], I32, name="word_window", offset=24576)
         nc.sync.dma_start(word_window[:], tab_words[0].rearrange("p t i -> p (t i)").bitcast(I32))
         dn_raw = load_words(dn_words, "dn_raw", 57344)
         wb_raw = load_words(wb_words, "wb_raw", 77824)
         bias = keep.tile([P, PACK], F32, name="bias")
-        nc.sync.dma_start(bias[:], b.rearrange("(p t) -> p t", t=PACK))
+        nc.scalar.dma_start(bias[:], b.rearrange("(p t) -> p t", t=PACK))
 
         nc.vector.memset(weight_scales[0:ROW0].bitcast(I32), 0)
         nc.vector.memset(scale_window[0:ROW0, :].bitcast(I32), 0)
@@ -219,19 +219,20 @@ def tile_list_xcross_noneP_kernel(
                 cols = slice(STORE_AFTER[i], starts[i] + PIECES[i])
                 nc.sync.dma_start(code_rows[:, cols], out_codes[:, cols])
 
-        for i in range(len(PIECES)):
-            piece = slice(starts[i], starts[i] + PIECES[i])
+        pieces = [slice(starts[i], starts[i] + PIECES[i]) for i in range(len(PIECES))]
+        for i in (0, 1, 3, 2):
             nc.vector.tensor_tensor(
-                high[:, 1, piece], x0[3][:].indirect(entries(starts[i], PIECES[i])), factor[:, piece], MULT
+                high[:, 1, pieces[i]], x0[3][:].indirect(entries(starts[i], PIECES[i])), factor[:, pieces[i]], MULT
             )
-            if i in STORE_AFTER:
-                cols = slice(STORE_AFTER[i], starts[i] + PIECES[i])
-                nc.sync.dma_start(out_rows[:, 3, cols], high[:, 1, cols])
-            copy = nc.vector.tensor_copy if i == len(PIECES) - 1 else nc.scalar.copy
-            copy(rounded[i][:, :, 2:4], high[:, :, piece].rearrange("p t j -> p j t"))
             if i > 0:
-                quantise(i - 1)
-        quantise(len(PIECES) - 1)
+                cols = slice(0 if i == 1 else starts[i], starts[i] + PIECES[i])
+                nc.sync.dma_start(out_rows[:, 3, cols], high[:, 1, cols])
+        for i in (0, 1, 3):
+            nc.scalar.copy(rounded[i][:, :, 2:4], high[:, :, pieces[i]].rearrange("p t j -> p j t"))
+        quantise(0)
+        nc.vector.tensor_copy(rounded[2][:, :, 2:4], high[:, :, pieces[2]].rearrange("p t j -> p j t"))
+        for i in range(1, len(PIECES)):
+            quantise(i)
         for quad in range(4):
             queue = nc.scalar if quad % 2 else nc.sync
             queue.dma_start(

@@ -24,7 +24,7 @@ ROW0 = 96
 HALF = 512
 CHUNK = 128
 PIECES = (256, 256, 256, 256)
-STORE_AFTER = {1: 0, 2: 512, 3: 768}
+STORE_AFTER = {1: 0, 3: 512}
 
 
 def tile_list_xcross_noneP_kernel(
@@ -224,8 +224,8 @@ def tile_list_xcross_noneP_kernel(
             nc.vector.tensor_tensor(
                 high[:, 1, pieces[i]], x0[3][:].indirect(entries(starts[i], PIECES[i])), factor[:, pieces[i]], MULT
             )
-            if i > 0:
-                cols = slice(0 if i == 1 else starts[i], starts[i] + PIECES[i])
+            if i in (1, 2):
+                cols = slice(0, HALF) if i == 1 else slice(HALF, J)
                 nc.sync.dma_start(out_rows[:, 3, cols], high[:, 1, cols])
         for i in (0, 1, 3):
             nc.scalar.copy(rounded[i][:, :, 2:4], high[:, :, pieces[i]].rearrange("p t j -> p j t"))

@@ -20,7 +20,7 @@ IDENTITY = mybir.ActivationFunctionType.Identity
 P = 128
 PACK = 4
 PASSES = K // (P * PACK)
-ROW0 = 96
+SPREAD = 4
 HALF = 512
 CHUNK = 128
 PIECES = (256, 256, 256, 256)
@@ -44,8 +44,8 @@ def tile_list_xcross_noneP_kernel(
             nc.sync.dma_start(raw[:], words.rearrange("a p n i -> p a (n i)").bitcast(I32))
             return raw
 
-        def deal_words(raw, name):
-            dealt = keep.tile([P, PASSES, PACK, P], I32, name=name, align_bytes=64)
+        def deal_words(raw, name, offset):
+            dealt = placed.tile([P, PASSES, PACK, P], I32, name=name, align_bytes=64, offset=offset)
             nc.vector.tensor_copy(
                 dealt[:].rearrange("p a t m -> p a m t"), raw[:].rearrange("p a (m t) -> p a m t", t=PACK)
             )
@@ -61,52 +61,52 @@ def tile_list_xcross_noneP_kernel(
         offsets = keep.tile([P, J // 16], U16, name="offsets")
         nc.sync.dma_start(offsets[:], offs)
 
-        scale_window = keep.tile([P, T], U8, name="scale_window")
-        weight_scales = keep.tile([P, 2, N], U8, name="weight_scales")
-        nc.scalar.dma_start(weight_scales[ROW0:P, 0, :].bitcast(I32), dn_scales.rearrange("a q n -> q a n").bitcast(I32))
-        nc.scalar.dma_start(weight_scales[ROW0:P, 1, :].bitcast(I32), wb_scales.rearrange("a q n -> q a n").bitcast(I32))
-        nc.sync.dma_start(scale_window[ROW0:P, :].bitcast(I32), tab_scales.rearrange("a q c -> q a c").bitcast(I32))
-        word_window = placed.tile([P, T], I32, name="word_window", offset=24576)
+        scale_window = placed.tile([P, T], U8, name="scale_window", offset=0)
+        weight_scales = placed.tile([P, 2, N], U8, name="weight_scales", offset=4096)
+        nc.vector.memset(scale_window[:].bitcast(I32), 0)
+        nc.vector.memset(weight_scales[:].bitcast(I32), 0)
+        nc.gpsimd.dma_start(scale_window[0:P:SPREAD, :].bitcast(I32), tab_scales.rearrange("a q c -> q a c").bitcast(I32))
+        nc.gpsimd.dma_start(weight_scales[0:P:SPREAD, 0, :].bitcast(I32), dn_scales.rearrange("a q n -> q a n").bitcast(I32))
+        nc.gpsimd.dma_start(weight_scales[0:P:SPREAD, 1, :].bitcast(I32), wb_scales.rearrange("a q n -> q a n").bitcast(I32))
+        word_window = placed.tile([P, T], I32, name="word_window", offset=12288)
         nc.sync.dma_start(word_window[:], tab_words[0].rearrange("p t i -> p (t i)").bitcast(I32))
-        dn_raw = load_words(dn_words, "dn_raw", 57344)
-        wb_raw = load_words(wb_words, "wb_raw", 77824)
+        dn_raw = load_words(dn_words, "dn_raw", 8192)
+        wb_raw = load_words(wb_words, "wb_raw", 45056)
+        up_raw = placed.tile([P, PACK, N], F32, name="up_raw", offset=28672)
+        nc.sync.dma_start(up_raw[:], upw.rearrange("(p i) n -> p i n", i=PACK))
+        x0 = [load_x0(0, 61440)]
         bias = keep.tile([P, PACK], F32, name="bias")
         nc.scalar.dma_start(bias[:], b.rearrange("(p t) -> p t", t=PACK))
 
-        nc.vector.memset(weight_scales[0:ROW0].bitcast(I32), 0)
-        nc.vector.memset(scale_window[0:ROW0, :].bitcast(I32), 0)
         planes = keep.tile([P, PASSES, J + 2 * N], U8, name="planes", align_bytes=64)
         nc.vector.memset(planes[:].bitcast(I32), 0)
 
         bias_one = keep.tile([P, PACK], F32, name="bias_one")
         nc.scalar.activation(bias_one[:], bias[:], IDENTITY, bias=1.0)
 
-        scale_rows = keep.tile([P, J + 2 * N], U8, name="scale_rows")
+        picked_scales = keep.tile([P, J], U8, name="picked_scales")
+        nc.vector.tensor_copy(picked_scales[:], scale_window[:].indirect(offsets[:]))
+        scale_rows = placed.tile([P, J + 2 * N], U8, name="scale_rows", offset=0)
+        nc.vector.tensor_copy(scale_rows[:, 0:J].bitcast(I32), picked_scales[:].bitcast(I32))
         nc.vector.tensor_copy(
             scale_rows[:, J:].rearrange("p (w t m) -> p w t m", w=2, t=PACK),
             weight_scales[:].rearrange("p w (m t) -> p w t m", t=PACK),
         )
-        picked_scales = placed.tile([P, J], U8, name="picked_scales", offset=7680)
-        nc.vector.tensor_copy(picked_scales[:], scale_window[:].indirect(offsets[:]))
-        nc.vector.tensor_copy(scale_rows[:, 0:J].bitcast(I32), picked_scales[:].bitcast(I32))
         for quad in (0, 2, 1, 3):
-            nc.sync.dma_start(
+            nc.scalar.dma_start(
                 planes[32 * quad : 32 * quad + 4].bitcast(I32),
-                scale_rows[ROW0 + 8 * quad : ROW0 + 8 * quad + 8, :].bitcast(I32),
+                scale_rows[32 * quad : 32 * quad + 32 : SPREAD, :].bitcast(I32),
             )
-        up_raw = placed.tile([P, PACK, N], F32, name="up_raw", offset=0)
-        nc.sync.dma_start(up_raw[:], upw.rearrange("(p i) n -> p i n", i=PACK))
-        x0 = [load_x0(0, 8192)]
 
         def gather_words(half):
-            picked = placed.tile([P, HALF], U32, name="picked%d" % half, offset=(40960, 60416)[half])
+            picked = placed.tile([P, HALF], U32, name="picked%d" % half, offset=(4096, 8192)[half])
             nc.vector.tensor_copy(picked[:], word_window[:].bitcast(U32).indirect(entries(half * HALF, HALF)))
             parted = keep.tile([P, PASSES, HALF], U16, name="parted%d" % half, align_bytes=64)
             nc.vector.tensor_copy(parted[:], picked[:].bitcast(U16).rearrange("p (j a) -> p a j", a=PASSES))
             return parted
 
         def first_stage(half):
-            rounded = keep.tile([P, HALF, PACK], BF16, name="h_rounded%d" % half, align_bytes=64)
+            rounded = placed.tile([P, HALF, PACK], BF16, name="h_rounded%d" % half, align_bytes=64, offset=77824 + 4096 * half)
             for c0 in range(0, HALF, CHUNK):
                 bank = psum.tile([P, PACK, CHUNK], F32, name="h_bank", tag="bank")
                 for t in range(PACK):
@@ -129,20 +129,20 @@ def tile_list_xcross_noneP_kernel(
             return codes, scales
 
         v_codes = [gather_words(0)]
-        x0.append(load_x0(1, 40960))
-        dn_codes = deal_words(dn_raw, "dn_codes")
+        dn_codes = deal_words(dn_raw, "dn_codes", 4096)
         v_codes.append(gather_words(1))
-        x0.append(load_x0(2, 24576))
-        x0.append(load_x0(3, 61440))
-        wb_codes = deal_words(wb_raw, "wb_codes")
+        x0.append(load_x0(1, 12288))
+        wb_codes = deal_words(wb_raw, "wb_codes", 8192)
 
-        up_rounded = keep.tile([P, N * PACK], BF16, name="up_rounded", align_bytes=64)
+        up_rounded = placed.tile([P, N * PACK], BF16, name="up_rounded", align_bytes=64, offset=45056)
         up_dealt = up_rounded[:].rearrange("p (t m i) -> p m t i", t=PACK, i=PACK)
         up_source = up_raw[:].rearrange("p i (m t) -> p m t i", t=PACK)
         nc.vector.tensor_copy(up_dealt, up_source)
         up_codes = keep.tile([P, N], I32, name="up_codes", align_bytes=64)
         up_planes = keep.tile([P, N], U8, name="up_planes", align_bytes=64)
         nc.vector.quantize_mx(out=up_codes[:].bitcast(FP8X4), scales=up_planes[:], in_=up_rounded[:])
+        x0.append(load_x0(2, 28672))
+        x0.append(load_x0(3, 45056))
 
         def second_stage(t, half):
             h_codes, h_scales = h[half]
@@ -178,7 +178,7 @@ def tile_list_xcross_noneP_kernel(
         ]
 
         h = [first_stage(half) for half in range(2)]
-        y = {(t, half): second_stage(t, half) for t, half in ((0, 0), (1, 0), (0, 1), (1, 1), (2, 0), (2, 1), (3, 0), (3, 1))}
+        y = {(t, half): second_stage(t, half) for half in range(2) for t in range(PACK)}
 
         def make_factor(t):
             made = keep.tile([P, J], F32, name="factor%d" % t)
@@ -188,7 +188,7 @@ def tile_list_xcross_noneP_kernel(
                 )
             return made
 
-        x0_picked = keep.tile([P, J], F32, name="x0_picked")
+        x0_picked = placed.tile([P, J], F32, name="x0_picked", offset=77824)
         nc.vector.tensor_copy(x0_picked[:], x0[0][:].indirect(offsets[:]))
         for half in range(2):
             cols = slice(half * HALF, (half + 1) * HALF)

@@ -34,7 +34,7 @@ def tile_list_xcross_noneP_kernel(
     with ExitStack() as ctx:
         keep = ctx.enter_context(tc.tile_pool(name="keep", bufs=1))
         placed = ctx.enter_context(tc.tile_pool(name="placed", bufs=1))
-        psum = ctx.enter_context(tc.psum_pool(name="psum", bufs=8))
+        psum = ctx.enter_context(tc.psum_pool(name="psum", bufs=4))
 
         def entries(j0, width):
             return offsets[:, j0 // 16 : (j0 + width) // 16]
@@ -51,6 +51,11 @@ def tile_list_xcross_noneP_kernel(
             )
             return dealt
 
+        def load_up(pair, offset):
+            raw = placed.tile([P, 2, N], F32, name="up_raw%d" % pair, offset=offset)
+            nc.sync.dma_start(raw[:], upw.rearrange("(p i) n -> p i n", i=PACK)[:, 2 * pair : 2 * pair + 2, :])
+            return raw
+
         x0_rows = x0T.rearrange("(p t) c -> p t c", t=PACK)
 
         def load_x0(t, offset):
@@ -61,52 +66,58 @@ def tile_list_xcross_noneP_kernel(
         offsets = keep.tile([P, J // 16], U16, name="offsets")
         nc.sync.dma_start(offsets[:], offs)
 
-        scale_window = placed.tile([P, T], U8, name="scale_window", offset=0)
-        weight_scales = placed.tile([P, 2, N], U8, name="weight_scales", offset=4096)
-        nc.vector.memset(scale_window[:].bitcast(I32), 0)
-        nc.vector.memset(weight_scales[:].bitcast(I32), 0)
-        nc.gpsimd.dma_start(scale_window[0:P:SPREAD, :].bitcast(I32), tab_scales.rearrange("a q c -> q a c").bitcast(I32))
-        nc.gpsimd.dma_start(weight_scales[0:P:SPREAD, 0, :].bitcast(I32), dn_scales.rearrange("a q n -> q a n").bitcast(I32))
-        nc.gpsimd.dma_start(weight_scales[0:P:SPREAD, 1, :].bitcast(I32), wb_scales.rearrange("a q n -> q a n").bitcast(I32))
-        word_window = placed.tile([P, T], I32, name="word_window", offset=12288)
-        nc.sync.dma_start(word_window[:], tab_words[0].rearrange("p t i -> p (t i)").bitcast(I32))
-        dn_raw = load_words(dn_words, "dn_raw", 8192)
-        wb_raw = load_words(wb_words, "wb_raw", 45056)
-        up_raw = placed.tile([P, PACK, N], F32, name="up_raw", offset=28672)
-        nc.sync.dma_start(up_raw[:], upw.rearrange("(p i) n -> p i n", i=PACK))
-        x0 = [load_x0(0, 61440)]
-        bias = keep.tile([P, PACK], F32, name="bias")
-        nc.scalar.dma_start(bias[:], b.rearrange("(p t) -> p t", t=PACK))
+        bias = placed.tile([P, 2 * PACK * PACK], F32, name="bias", offset=36864 - 64)
+        nc.sync.dma_start(bias[:, 0:PACK], b.rearrange("(p t) -> p t", t=PACK))
+        dn_raw = load_words(dn_words, "dn_raw", 77824)
+        wb_raw = load_words(wb_words, "wb_raw", 81920)
 
+        scale_window = placed.tile([P, T], U8, name="scale_window", offset=40960)
+        weight_scales = keep.tile([P, 2, N], U8, name="weight_scales")
+        nc.vector.memset(weight_scales[:].bitcast(I32), 0)
+        nc.vector.memset(scale_window[:].bitcast(I32), 0)
+        nc.sync.dma_start(weight_scales[0:P:SPREAD, 0, :].bitcast(I32), dn_scales.rearrange("a q n -> q a n").bitcast(I32))
+        nc.sync.dma_start(weight_scales[0:P:SPREAD, 1, :].bitcast(I32), wb_scales.rearrange("a q n -> q a n").bitcast(I32))
+        nc.sync.dma_start(scale_window[0:P:SPREAD, :].bitcast(I32), tab_scales.rearrange("a q c -> q a c").bitcast(I32))
         planes = keep.tile([P, PASSES, J + 2 * N], U8, name="planes", align_bytes=64)
         nc.vector.memset(planes[:].bitcast(I32), 0)
 
         bias_one = keep.tile([P, PACK], F32, name="bias_one")
-        nc.scalar.activation(bias_one[:], bias[:], IDENTITY, bias=1.0)
+        nc.vector.tensor_scalar_add(bias_one[:], bias[:, 0:PACK], 1.0)
+        word_window = placed.tile([P, T], I32, name="word_window", offset=20480)
+        nc.sync.dma_start(word_window[:], tab_words[0].rearrange("p t i -> p (t i)").bitcast(I32))
+        up_raw = [load_up(0, 36864)]
+        dn_codes = deal_words(dn_raw, "dn_codes", 86016)
 
-        picked_scales = keep.tile([P, J], U8, name="picked_scales")
-        nc.vector.tensor_copy(picked_scales[:], scale_window[:].indirect(offsets[:]))
-        scale_rows = placed.tile([P, J + 2 * N], U8, name="scale_rows", offset=0)
-        nc.vector.tensor_copy(scale_rows[:, 0:J].bitcast(I32), picked_scales[:].bitcast(I32))
+        scale_rows = keep.tile([P, J + 2 * N], U8, name="scale_rows")
         nc.vector.tensor_copy(
             scale_rows[:, J:].rearrange("p (w t m) -> p w t m", w=2, t=PACK),
             weight_scales[:].rearrange("p w (m t) -> p w t m", t=PACK),
         )
+        picked_scales = placed.tile([P, J], U8, name="picked_scales", offset=61440 - 512)
+        nc.vector.tensor_copy(picked_scales[:], scale_window[:].indirect(offsets[:]))
+        nc.vector.tensor_copy(scale_rows[:, 0:J].bitcast(I32), picked_scales[:].bitcast(I32))
         for quad in (0, 2, 1, 3):
-            nc.scalar.dma_start(
+            nc.sync.dma_start(
                 planes[32 * quad : 32 * quad + 4].bitcast(I32),
                 scale_rows[32 * quad : 32 * quad + 32 : SPREAD, :].bitcast(I32),
             )
+        wb_codes = deal_words(wb_raw, "wb_codes", 40960)
+        up_raw.append(load_up(1, 57344))
+        x0 = [load_x0(0, 61440)]
+
+        up_rounded = placed.tile([P, N * PACK], BF16, name="up_rounded", align_bytes=64, offset=98304)
+        up_dealt = up_rounded[:].rearrange("p (t m i) -> p m t i", t=PACK, i=PACK)
+        nc.scalar.copy(up_dealt[:, :, :, 0:2], up_raw[0][:].rearrange("p i (m t) -> p m t i", t=PACK))
 
         def gather_words(half):
-            picked = placed.tile([P, HALF], U32, name="picked%d" % half, offset=(4096, 8192)[half])
+            picked = placed.tile([P, HALF], U32, name="picked%d" % half, offset=(4096 - 1024, 2048)[half])
             nc.vector.tensor_copy(picked[:], word_window[:].bitcast(U32).indirect(entries(half * HALF, HALF)))
             parted = keep.tile([P, PASSES, HALF], U16, name="parted%d" % half, align_bytes=64)
             nc.vector.tensor_copy(parted[:], picked[:].bitcast(U16).rearrange("p (j a) -> p a j", a=PASSES))
             return parted
 
         def first_stage(half):
-            rounded = placed.tile([P, HALF, PACK], BF16, name="h_rounded%d" % half, align_bytes=64, offset=77824 + 4096 * half)
+            rounded = placed.tile([P, HALF, PACK], BF16, name="h_rounded%d" % half, align_bytes=64, offset=90112 + 4096 * half)
             for c0 in range(0, HALF, CHUNK):
                 bank = psum.tile([P, PACK, CHUNK], F32, name="h_bank", tag="bank")
                 for t in range(PACK):
@@ -129,20 +140,14 @@ def tile_list_xcross_noneP_kernel(
             return codes, scales
 
         v_codes = [gather_words(0)]
-        dn_codes = deal_words(dn_raw, "dn_codes", 4096)
+        x0.append(load_x0(1, 4096))
         v_codes.append(gather_words(1))
-        x0.append(load_x0(1, 12288))
-        wb_codes = deal_words(wb_raw, "wb_codes", 8192)
-
-        up_rounded = placed.tile([P, N * PACK], BF16, name="up_rounded", align_bytes=64, offset=45056)
-        up_dealt = up_rounded[:].rearrange("p (t m i) -> p m t i", t=PACK, i=PACK)
-        up_source = up_raw[:].rearrange("p i (m t) -> p m t i", t=PACK)
-        nc.vector.tensor_copy(up_dealt, up_source)
-        up_codes = keep.tile([P, N], I32, name="up_codes", align_bytes=64)
+        x0.append(load_x0(2, 20480))
+        nc.vector.tensor_copy(up_dealt[:, :, :, 2:4], up_raw[1][:].rearrange("p i (m t) -> p m t i", t=PACK))
+        up_codes = placed.tile([P, N], I32, name="up_codes", align_bytes=64, offset=1024)
         up_planes = keep.tile([P, N], U8, name="up_planes", align_bytes=64)
         nc.vector.quantize_mx(out=up_codes[:].bitcast(FP8X4), scales=up_planes[:], in_=up_rounded[:])
-        x0.append(load_x0(2, 28672))
-        x0.append(load_x0(3, 45056))
+        x0.append(load_x0(3, 98304))
 
         def second_stage(t, half):
             h_codes, h_scales = h[half]
@@ -169,40 +174,41 @@ def tile_list_xcross_noneP_kernel(
             return bank
 
         out_rows = out_0.rearrange("(p t) j -> p t j", t=PACK)
-        low = keep.tile([P, 2, J], F32, name="low")
-        high = keep.tile([P, 2, J], F32, name="high")
+        crossed = keep.tile([P, PACK, J], F32, name="crossed")
+        low = crossed[:, 0:2, :]
+        high = crossed[:, 2:4, :]
         starts = [sum(PIECES[:i]) for i in range(len(PIECES))]
         rounded = [
-            keep.tile([P, width, PACK], BF16, name="out_rounded%d" % i, align_bytes=64)
+            placed.tile([P, width, PACK], BF16, name="out_rounded%d" % i, align_bytes=64, offset=114688 + 2048 * i)
             for i, width in enumerate(PIECES)
         ]
 
         h = [first_stage(half) for half in range(2)]
-        y = {(t, half): second_stage(t, half) for half in range(2) for t in range(PACK)}
+        y = {(t, half): second_stage(t, half) for t, half in ((0, 0), (1, 0), (0, 1), (1, 1))}
+
+        halves = [slice(0, HALF), slice(HALF, J)]
 
         def make_factor(t):
-            made = keep.tile([P, J], F32, name="factor%d" % t)
+            made = placed.tile([P, J], F32, name="factor%d" % t, offset=(124928, 129024, 120832, 133120)[t])
             for half in range(2):
-                nc.scalar.activation(
-                    made[:, half * HALF : (half + 1) * HALF], y[t, half][:], IDENTITY, bias=bias_one[:, t : t + 1]
-                )
+                bank = y[t, half] if (t, half) in y else second_stage(t, half)
+                nc.scalar.activation(made[:, halves[half]], bank[:], IDENTITY, bias=bias_one[:, t : t + 1])
             return made
 
-        x0_picked = placed.tile([P, J], F32, name="x0_picked", offset=77824)
-        nc.vector.tensor_copy(x0_picked[:], x0[0][:].indirect(offsets[:]))
+        factors = [make_factor(t) for t in range(PACK)]
+        factor = factors[3]
         for half in range(2):
-            cols = slice(half * HALF, (half + 1) * HALF)
-            nc.vector.scalar_tensor_tensor(low[:, 0, cols], y[0, half][:], bias_one[:, 0:1], x0_picked[:, cols], ADD, MULT)
-        factors = [make_factor(t) for t in (1, 2, 3)]
-        factor = factors[2]
-        nc.vector.tensor_tensor(low[:, 1, :], x0[1][:].indirect(offsets[:]), factors[0][:], MULT)
-        nc.sync.dma_start(out_rows[:, 0:2, :], low[:])
-        for i in range(len(PIECES)):
+            for t in range(2):
+                nc.vector.tensor_tensor(
+                    crossed[:, t, halves[half]], x0[t][:].indirect(entries(half * HALF, HALF)), factors[t][:, halves[half]], MULT
+                )
+        for i in range(len(PIECES) - 1):
             nc.scalar.copy(
                 rounded[i][:, :, 0:2], low[:, :, starts[i] : starts[i] + PIECES[i]].rearrange("p t j -> p j t")
             )
-        nc.vector.tensor_tensor(high[:, 0, :], x0[2][:].indirect(offsets[:]), factors[1][:], MULT)
-        nc.sync.dma_start(out_rows[:, 2, :], high[:, 0, :])
+        nc.vector.tensor_tensor(high[:, 0, :], x0[2][:].indirect(offsets[:]), factors[2][:], MULT)
+        nc.vector.tensor_copy(rounded[3][:, :, 0:2], low[:, :, starts[3] :].rearrange("p t j -> p j t"))
+        nc.sync.dma_start(out_rows[:, 0:3, :], crossed[:, 0:3, :])
 
         out_codes = keep.tile([P, J], I32, name="out_codes", align_bytes=64)
         out_scales = keep.tile([P, J], U8, name="out_scales", align_bytes=64)

@@ -51,11 +51,6 @@ def tile_list_xcross_noneP_kernel(
             )
             return dealt
 
-        def load_up(pair, offset):
-            raw = placed.tile([P, 2, N], F32, name="up_raw%d" % pair, offset=offset)
-            nc.sync.dma_start(raw[:], upw.rearrange("(p i) n -> p i n", i=PACK)[:, 2 * pair : 2 * pair + 2, :])
-            return raw
-
         x0_rows = x0T.rearrange("(p t) c -> p t c", t=PACK)
 
         def load_x0(t, offset):
@@ -71,7 +66,7 @@ def tile_list_xcross_noneP_kernel(
         dn_raw = load_words(dn_words, "dn_raw", 77824)
         wb_raw = load_words(wb_words, "wb_raw", 81920)
 
-        scale_window = placed.tile([P, T], U8, name="scale_window", offset=40960)
+        scale_window = placed.tile([P, T], U8, name="scale_window", offset=98304)
         weight_scales = keep.tile([P, 2, N], U8, name="weight_scales")
         nc.vector.memset(weight_scales[:].bitcast(I32), 0)
         nc.vector.memset(scale_window[:].bitcast(I32), 0)
@@ -85,7 +80,8 @@ def tile_list_xcross_noneP_kernel(
         nc.vector.tensor_scalar_add(bias_one[:], bias[:, 0:PACK], 1.0)
         word_window = placed.tile([P, T], I32, name="word_window", offset=20480)
         nc.sync.dma_start(word_window[:], tab_words[0].rearrange("p t i -> p (t i)").bitcast(I32))
-        up_raw = [load_up(0, 36864)]
+        up_raw = placed.tile([P, PACK, N], F32, name="up_raw", offset=36864)
+        nc.sync.dma_start(up_raw[:], upw.rearrange("(p i) n -> p i n", i=PACK))
         dn_codes = deal_words(dn_raw, "dn_codes", 86016)
 
         scale_rows = keep.tile([P, J + 2 * N], U8, name="scale_rows")
@@ -101,13 +97,11 @@ def tile_list_xcross_noneP_kernel(
                 planes[32 * quad : 32 * quad + 4].bitcast(I32),
                 scale_rows[32 * quad : 32 * quad + 32 : SPREAD, :].bitcast(I32),
             )
-        wb_codes = deal_words(wb_raw, "wb_codes", 40960)
-        up_raw.append(load_up(1, 57344))
+        wb_codes = deal_words(wb_raw, "wb_codes", 98304)
         x0 = [load_x0(0, 61440)]
 
-        up_rounded = placed.tile([P, N * PACK], BF16, name="up_rounded", align_bytes=64, offset=98304)
+        up_rounded = placed.tile([P, N * PACK], BF16, name="up_rounded", align_bytes=64, offset=0)
         up_dealt = up_rounded[:].rearrange("p (t m i) -> p m t i", t=PACK, i=PACK)
-        nc.scalar.copy(up_dealt[:, :, :, 0:2], up_raw[0][:].rearrange("p i (m t) -> p m t i", t=PACK))
 
         def gather_words(half):
             picked = placed.tile([P, HALF], U32, name="picked%d" % half, offset=(4096 - 1024, 2048)[half])
@@ -143,11 +137,11 @@ def tile_list_xcross_noneP_kernel(
         x0.append(load_x0(1, 4096))
         v_codes.append(gather_words(1))
         x0.append(load_x0(2, 20480))
-        nc.vector.tensor_copy(up_dealt[:, :, :, 2:4], up_raw[1][:].rearrange("p i (m t) -> p m t i", t=PACK))
-        up_codes = placed.tile([P, N], I32, name="up_codes", align_bytes=64, offset=1024)
+        nc.vector.tensor_copy(up_dealt, up_raw[:].rearrange("p i (m t) -> p m t i", t=PACK))
+        up_codes = keep.tile([P, N], I32, name="up_codes", align_bytes=64)
         up_planes = keep.tile([P, N], U8, name="up_planes", align_bytes=64)
         nc.vector.quantize_mx(out=up_codes[:].bitcast(FP8X4), scales=up_planes[:], in_=up_rounded[:])
-        x0.append(load_x0(3, 98304))
+        x0.append(load_x0(3, 36864))
 
         def second_stage(t, half):
             h_codes, h_scales = h[half]
@@ -179,7 +173,7 @@ def tile_list_xcross_noneP_kernel(
         high = crossed[:, 2:4, :]
         starts = [sum(PIECES[:i]) for i in range(len(PIECES))]
         rounded = [
-            placed.tile([P, width, PACK], BF16, name="out_rounded%d" % i, align_bytes=64, offset=114688 + 2048 * i)
+            keep.tile([P, width, PACK], BF16, name="out_rounded%d" % i, align_bytes=64)
             for i, width in enumerate(PIECES)
         ]
 
@@ -189,7 +183,7 @@ def tile_list_xcross_noneP_kernel(
         halves = [slice(0, HALF), slice(HALF, J)]
 
         def make_factor(t):
-            made = placed.tile([P, J], F32, name="factor%d" % t, offset=(124928, 129024, 120832, 133120)[t])
+            made = keep.tile([P, J], F32, name="factor%d" % t)
             for half in range(2):
                 bank = y[t, half] if (t, half) in y else second_stage(t, half)
                 nc.scalar.activation(made[:, halves[half]], bank[:], IDENTITY, bias=bias_one[:, t : t + 1])
@@ -202,13 +196,13 @@ def tile_list_xcross_noneP_kernel(
                 nc.vector.tensor_tensor(
                     crossed[:, t, halves[half]], x0[t][:].indirect(entries(half * HALF, HALF)), factors[t][:, halves[half]], MULT
                 )
-        for i in range(len(PIECES) - 1):
+        nc.sync.dma_start(out_rows[:, 0:2, :], low)
+        for i in range(len(PIECES)):
             nc.scalar.copy(
                 rounded[i][:, :, 0:2], low[:, :, starts[i] : starts[i] + PIECES[i]].rearrange("p t j -> p j t")
             )
         nc.vector.tensor_tensor(high[:, 0, :], x0[2][:].indirect(offsets[:]), factors[2][:], MULT)
-        nc.vector.tensor_copy(rounded[3][:, :, 0:2], low[:, :, starts[3] :].rearrange("p t j -> p j t"))
-        nc.sync.dma_start(out_rows[:, 0:3, :], crossed[:, 0:3, :])
+        nc.sync.dma_start(out_rows[:, 2, :], high[:, 0, :])
 
         out_codes = keep.tile([P, J], I32, name="out_codes", align_bytes=64)
         out_scales = keep.tile([P, J], U8, name="out_scales", align_bytes=64)

@@ -196,13 +196,12 @@ def tile_list_xcross_noneP_kernel(
                 nc.vector.tensor_tensor(
                     crossed[:, t, halves[half]], x0[t][:].indirect(entries(half * HALF, HALF)), factors[t][:, halves[half]], MULT
                 )
-        nc.sync.dma_start(out_rows[:, 0:2, :], low)
         for i in range(len(PIECES)):
             nc.scalar.copy(
                 rounded[i][:, :, 0:2], low[:, :, starts[i] : starts[i] + PIECES[i]].rearrange("p t j -> p j t")
             )
         nc.vector.tensor_tensor(high[:, 0, :], x0[2][:].indirect(offsets[:]), factors[2][:], MULT)
-        nc.sync.dma_start(out_rows[:, 2, :], high[:, 0, :])
+        nc.sync.dma_start(out_rows[:, 0:3, :], crossed[:, 0:3, :])
 
         out_codes = keep.tile([P, J], I32, name="out_codes", align_bytes=64)
         out_scales = keep.tile([P, J], U8, name="out_scales", align_bytes=64)

@@ -64,7 +64,6 @@ def tile_list_xcross_noneP_kernel(
         bias = placed.tile([P, 2 * PACK * PACK], F32, name="bias", offset=36864 - 64)
         nc.sync.dma_start(bias[:, 0:PACK], b.rearrange("(p t) -> p t", t=PACK))
         dn_raw = load_words(dn_words, "dn_raw", 77824)
-        wb_raw = load_words(wb_words, "wb_raw", 81920)
 
         scale_window = placed.tile([P, T], U8, name="scale_window", offset=98304)
         weight_scales = keep.tile([P, 2, N], U8, name="weight_scales")
@@ -72,6 +71,7 @@ def tile_list_xcross_noneP_kernel(
         nc.vector.memset(scale_window[:].bitcast(I32), 0)
         nc.sync.dma_start(weight_scales[0:P:SPREAD, 0, :].bitcast(I32), dn_scales.rearrange("a q n -> q a n").bitcast(I32))
         nc.sync.dma_start(weight_scales[0:P:SPREAD, 1, :].bitcast(I32), wb_scales.rearrange("a q n -> q a n").bitcast(I32))
+        wb_raw = load_words(wb_words, "wb_raw", 81920)
         nc.sync.dma_start(scale_window[0:P:SPREAD, :].bitcast(I32), tab_scales.rearrange("a q c -> q a c").bitcast(I32))
         planes = keep.tile([P, PASSES, J + 2 * N], U8, name="planes", align_bytes=64)
         nc.vector.memset(planes[:].bitcast(I32), 0)

@@ -111,7 +111,7 @@ def tile_list_xcross_noneP_kernel(
             return parted
 
         def first_stage(half):
-            rounded = placed.tile([P, HALF, PACK], BF16, name="h_rounded%d" % half, align_bytes=64, offset=90112 + 4096 * half)
+            rounded = placed.tile([P, HALF, PACK], BF16, name="h_rounded%d" % half, align_bytes=64, offset=(8192, 94208)[half])
             for c0 in range(0, HALF, CHUNK):
                 bank = psum.tile([P, PACK, CHUNK], F32, name="h_bank", tag="bank")
                 for t in range(PACK):
@@ -134,14 +134,12 @@ def tile_list_xcross_noneP_kernel(
             return codes, scales
 
         v_codes = [gather_words(0)]
-        x0.append(load_x0(1, 4096))
         v_codes.append(gather_words(1))
-        x0.append(load_x0(2, 20480))
+        x0.append(load_x0(1, 20480))
         nc.vector.tensor_copy(up_dealt, up_raw[:].rearrange("p i (m t) -> p m t i", t=PACK))
         up_codes = keep.tile([P, N], I32, name="up_codes", align_bytes=64)
         up_planes = keep.tile([P, N], U8, name="up_planes", align_bytes=64)
         nc.vector.quantize_mx(out=up_codes[:].bitcast(FP8X4), scales=up_planes[:], in_=up_rounded[:])
-        x0.append(load_x0(3, 36864))
 
         def second_stage(t, half):
             h_codes, h_scales = h[half]
@@ -177,25 +175,30 @@ def tile_list_xcross_noneP_kernel(
             for i, width in enumerate(PIECES)
         ]
 
-        h = [first_stage(half) for half in range(2)]
+        h = [first_stage(0)]
+        x0.append(load_x0(2, 4096))
+        h.append(first_stage(1))
         y = {(t, half): second_stage(t, half) for t, half in ((0, 0), (1, 0), (0, 1), (1, 1))}
 
         halves = [slice(0, HALF), slice(HALF, J)]
 
+        first = placed.tile([P, HALF], F32, name="first_factor", offset=45056)
+
         def make_factor(t):
             made = keep.tile([P, J], F32, name="factor%d" % t)
+            parts = [first[:] if (t, half) == (0, 0) else made[:, halves[half]] for half in range(2)]
             for half in range(2):
                 bank = y[t, half] if (t, half) in y else second_stage(t, half)
-                nc.scalar.activation(made[:, halves[half]], bank[:], IDENTITY, bias=bias_one[:, t : t + 1])
+                nc.scalar.activation(parts[half], bank[:], IDENTITY, bias=bias_one[:, t : t + 1])
             return made
 
         factors = [make_factor(t) for t in range(PACK)]
         factor = factors[3]
         for half in range(2):
             for t in range(2):
-                nc.vector.tensor_tensor(
-                    crossed[:, t, halves[half]], x0[t][:].indirect(entries(half * HALF, HALF)), factors[t][:, halves[half]], MULT
-                )
+                made = first[:] if (t, half) == (0, 0) else factors[t][:, halves[half]]
+                nc.vector.tensor_tensor(crossed[:, t, halves[half]], x0[t][:].indirect(entries(half * HALF, HALF)), made, MULT)
+        x0.append(load_x0(3, 36864))
         for i in range(len(PIECES)):
             nc.scalar.copy(
                 rounded[i][:, :, 0:2], low[:, :, starts[i] : starts[i] + PIECES[i]].rearrange("p t j -> p j t")

@@ -20,7 +20,8 @@ IDENTITY = mybir.ActivationFunctionType.Identity
 P = 128
 PACK = 4
 PASSES = K // (P * PACK)
-SPREAD = 4
+SPREAD = 3
+ROW0 = 32
 HALF = 512
 CHUNK = 128
 PIECES = (256, 256, 256, 256)
@@ -69,10 +70,10 @@ def tile_list_xcross_noneP_kernel(
         weight_scales = keep.tile([P, 2, N], U8, name="weight_scales")
         nc.vector.memset(weight_scales[:].bitcast(I32), 0)
         nc.vector.memset(scale_window[:].bitcast(I32), 0)
-        nc.sync.dma_start(weight_scales[0:P:SPREAD, 0, :].bitcast(I32), dn_scales.rearrange("a q n -> q a n").bitcast(I32))
-        nc.sync.dma_start(weight_scales[0:P:SPREAD, 1, :].bitcast(I32), wb_scales.rearrange("a q n -> q a n").bitcast(I32))
+        nc.sync.dma_start(weight_scales[ROW0:P:SPREAD, 0, :].bitcast(I32), dn_scales.rearrange("a q n -> q a n").bitcast(I32))
+        nc.sync.dma_start(weight_scales[ROW0:P:SPREAD, 1, :].bitcast(I32), wb_scales.rearrange("a q n -> q a n").bitcast(I32))
         wb_raw = load_words(wb_words, "wb_raw", 81920)
-        nc.sync.dma_start(scale_window[0:P:SPREAD, :].bitcast(I32), tab_scales.rearrange("a q c -> q a c").bitcast(I32))
+        nc.sync.dma_start(scale_window[ROW0:P:SPREAD, :].bitcast(I32), tab_scales.rearrange("a q c -> q a c").bitcast(I32))
         planes = keep.tile([P, PASSES, J + 2 * N], U8, name="planes", align_bytes=64)
         nc.vector.memset(planes[:].bitcast(I32), 0)
 
@@ -95,7 +96,7 @@ def tile_list_xcross_noneP_kernel(
         for quad in (0, 2, 1, 3):
             nc.sync.dma_start(
                 planes[32 * quad : 32 * quad + 4].bitcast(I32),
-                scale_rows[32 * quad : 32 * quad + 32 : SPREAD, :].bitcast(I32),
+                scale_rows[ROW0 + 8 * SPREAD * quad : ROW0 + 8 * SPREAD * (quad + 1) : SPREAD, :].bitcast(I32),
             )
         wb_codes = deal_words(wb_raw, "wb_codes", 98304)
         x0 = [load_x0(0, 61440)]

@@ -25,7 +25,6 @@ ROW0 = 32
 HALF = 512
 CHUNK = 128
 PIECES = (256, 256, 256, 256)
-STORE_AFTER = {1: 0, 3: 512}
 
 
 def tile_list_xcross_noneP_kernel(
@@ -204,38 +203,57 @@ def tile_list_xcross_noneP_kernel(
             nc.scalar.copy(
                 rounded[i][:, :, 0:2], low[:, :, starts[i] : starts[i] + PIECES[i]].rearrange("p t j -> p j t")
             )
-        nc.vector.tensor_tensor(high[:, 0, :], x0[2][:].indirect(offsets[:]), factors[2][:], MULT)
-        nc.sync.dma_start(out_rows[:, 0:3, :], crossed[:, 0:3, :])
+        flat_rows = out_0.rearrange("(p t) j -> p (t j)", t=PACK)
+        flat = crossed[:].rearrange("p t j -> p (t j)")
+
+        def store_rows(c0, c1):
+            nc.sync.dma_start(flat_rows[:, c0:c1], flat[:, c0:c1])
+
+        for half in range(2):
+            nc.vector.tensor_tensor(
+                high[:, 0, halves[half]], x0[2][:].indirect(entries(half * HALF, HALF)), factors[2][:, halves[half]], MULT
+            )
+            if half == 0:
+                store_rows(0, 2 * J + HALF)
 
         out_codes = keep.tile([P, J], I32, name="out_codes", align_bytes=64)
         out_scales = keep.tile([P, J], U8, name="out_scales", align_bytes=64)
         code_rows = out_1[0].rearrange("p j i -> p (j i)").bitcast(I32)
-
-        def quantise(i):
-            cols = slice(starts[i], starts[i] + PIECES[i])
-            nc.vector.quantize_mx(
-                out=out_codes[:, cols].bitcast(FP8X4),
-                scales=out_scales[:, cols],
-                in_=rounded[i][:].rearrange("p j t -> p (j t)"),
-            )
-            if i in STORE_AFTER:
-                cols = slice(STORE_AFTER[i], starts[i] + PIECES[i])
-                nc.sync.dma_start(code_rows[:, cols], out_codes[:, cols])
-
         pieces = [slice(starts[i], starts[i] + PIECES[i]) for i in range(len(PIECES))]
-        for i in (0, 1, 3, 2):
+
+        def cross(i):
             nc.vector.tensor_tensor(
                 high[:, 1, pieces[i]], x0[3][:].indirect(entries(starts[i], PIECES[i])), factor[:, pieces[i]], MULT
             )
-            if i in (1, 2):
-                cols = slice(0, HALF) if i == 1 else slice(HALF, J)
-                nc.sync.dma_start(out_rows[:, 3, cols], high[:, 1, cols])
+
+        def round_high(i, engine_copy):
+            engine_copy(rounded[i][:, :, 2:4], high[:, :, pieces[i]].rearrange("p t j -> p j t"))
+
+        def quantise(i):
+            nc.vector.quantize_mx(
+                out=out_codes[:, pieces[i]].bitcast(FP8X4),
+                scales=out_scales[:, pieces[i]],
+                in_=rounded[i][:].rearrange("p j t -> p (j t)"),
+            )
+
+        def store_codes(c0, c1):
+            nc.sync.dma_start(code_rows[:, c0:c1], out_codes[:, c0:c1])
+
+        cross(0)
+        cross(1)
+        store_rows(2 * J + HALF, 3 * J + HALF)
+        cross(3)
+        cross(2)
+        store_rows(3 * J + HALF, 4 * J)
         for i in (0, 1, 3):
-            nc.scalar.copy(rounded[i][:, :, 2:4], high[:, :, pieces[i]].rearrange("p t j -> p j t"))
+            round_high(i, nc.scalar.copy)
         quantise(0)
-        nc.vector.tensor_copy(rounded[2][:, :, 2:4], high[:, :, pieces[2]].rearrange("p t j -> p j t"))
-        for i in range(1, len(PIECES)):
-            quantise(i)
+        round_high(2, nc.vector.tensor_copy)
+        quantise(1)
+        store_codes(0, HALF)
+        quantise(2)
+        quantise(3)
+        store_codes(HALF, J)
         for quad in range(4):
             queue = nc.scalar if quad % 2 else nc.sync
             queue.dma_start(

@@ -36,6 +36,7 @@ def tile_list_xcross_noneP_kernel(
         placed = ctx.enter_context(tc.tile_pool(name="placed", bufs=1))
         psum = ctx.enter_context(tc.psum_pool(name="psum", bufs=4))
 
+
         def entries(j0, width):
             return offsets[:, j0 // 16 : (j0 + width) // 16]
 
@@ -46,8 +47,9 @@ def tile_list_xcross_noneP_kernel(
 
         def deal_words(raw, name, offset):
             dealt = placed.tile([P, PASSES, PACK, P], I32, name=name, align_bytes=64, offset=offset)
-            nc.vector.tensor_copy(
-                dealt[:].rearrange("p a t m -> p a m t"), raw[:].rearrange("p a (m t) -> p a m t", t=PACK)
+            nc.scalar.copy(
+                dealt[:].bitcast(U32).rearrange("p a t m -> p a t m"),
+                raw[:].bitcast(U32).rearrange("p a (m t) -> p a t m", t=PACK),
             )
             return dealt
 
@@ -68,11 +70,12 @@ def tile_list_xcross_noneP_kernel(
         scale_window = placed.tile([P, T], U8, name="scale_window", offset=98304)
         weight_scales = keep.tile([P, 2, N], U8, name="weight_scales")
         nc.vector.memset(weight_scales[:].bitcast(I32), 0)
-        nc.vector.memset(scale_window[:].bitcast(I32), 0)
+        nc.vector.memset(scale_window[:, 0 : T // 2].bitcast(I32), 0)
+        nc.gpsimd.memset(scale_window[:, T // 2 :].bitcast(I32), 0)
         nc.sync.dma_start(weight_scales[ROW0:P:SPREAD, 0, :].bitcast(I32), dn_scales.rearrange("a q n -> q a n").bitcast(I32))
         nc.sync.dma_start(weight_scales[ROW0:P:SPREAD, 1, :].bitcast(I32), wb_scales.rearrange("a q n -> q a n").bitcast(I32))
-        wb_raw = load_words(wb_words, "wb_raw", 81920)
         nc.sync.dma_start(scale_window[ROW0:P:SPREAD, :].bitcast(I32), tab_scales.rearrange("a q c -> q a c").bitcast(I32))
+        wb_raw = load_words(wb_words, "wb_raw", 81920)
         planes = keep.tile([P, PASSES, J + 2 * N], U8, name="planes", align_bytes=64)
         nc.vector.memset(planes[:].bitcast(I32), 0)
 

@@ -23,7 +23,7 @@ PASSES = K // (P * PACK)
 SPREAD = 3
 ROW0 = 32
 HALF = 512
-CHUNK = 128
+CHUNK = 256
 PIECES = (256, 256, 256, 256)
 
 
@@ -63,7 +63,7 @@ def tile_list_xcross_noneP_kernel(
         offsets = keep.tile([P, J // 16], U16, name="offsets")
         nc.sync.dma_start(offsets[:], offs)
 
-        bias = placed.tile([P, 2 * PACK * PACK], F32, name="bias", offset=36864 - 64)
+        bias = keep.tile([P, PACK], F32, name="bias")
         nc.sync.dma_start(bias[:, 0:PACK], b.rearrange("(p t) -> p t", t=PACK))
         dn_raw = load_words(dn_words, "dn_raw", 77824)
 
@@ -116,19 +116,20 @@ def tile_list_xcross_noneP_kernel(
         def first_stage(half):
             rounded = placed.tile([P, HALF, PACK], BF16, name="h_rounded%d" % half, align_bytes=64, offset=(8192, 94208)[half])
             for c0 in range(0, HALF, CHUNK):
-                bank = psum.tile([P, PACK, CHUNK], F32, name="h_bank", tag="bank")
-                for t in range(PACK):
-                    for a in range(PASSES):
-                        nc.tensor.matmul_mx(
-                            out=bank[:, t, :],
-                            lhsT=dn_codes[:, a, t, :].bitcast(FP8X4),
-                            lhsT_scale=planes[:, a, J + t * P : J + (t + 1) * P],
-                            rhs=v_codes[half][:, a, c0 : c0 + CHUNK].bitcast(FP4X4),
-                            rhs_scale=planes[:, a, half * HALF + c0 : half * HALF + c0 + CHUNK],
-                            start=(a == 0),
-                            stop=(a == PASSES - 1),
-                        )
-                nc.scalar.copy(rounded[:, c0 : c0 + CHUNK, :], bank[:].rearrange("p t j -> p j t"))
+                for t0, empty in ((0, nc.scalar.copy), (2, nc.vector.tensor_copy if half else nc.scalar.copy)):
+                    bank = psum.tile([P, 2, CHUNK], F32, name="h_bank", tag="bank")
+                    for t in range(t0, t0 + 2):
+                        for a in range(PASSES):
+                            nc.tensor.matmul_mx(
+                                out=bank[:, t - t0, :],
+                                lhsT=dn_codes[:, a, t, :].bitcast(FP8X4),
+                                lhsT_scale=planes[:, a, J + t * P : J + (t + 1) * P],
+                                rhs=v_codes[half][:, a, c0 : c0 + CHUNK].bitcast(FP4X4),
+                                rhs_scale=planes[:, a, half * HALF + c0 : half * HALF + c0 + CHUNK],
+                                start=(a == 0),
+                                stop=(a == PASSES - 1),
+                            )
+                    empty(rounded[:, c0 : c0 + CHUNK, t0 : t0 + 2], bank[:].rearrange("p t j -> p j t"))
             codes = keep.tile([P, HALF], I32, name="h_codes%d" % half, align_bytes=64)
             scales = keep.tile([P, HALF], U8, name="h_scales%d" % half, align_bytes=64)
             nc.vector.quantize_mx(

@@ -45,11 +45,11 @@ def tile_list_xcross_noneP_kernel(
             nc.sync.dma_start(raw[:], words.rearrange("a p n i -> p a (n i)").bitcast(I32))
             return raw
 
-        def deal_words(raw, name, offset):
+        def deal_words(raw, name, offset, engine_copy, view):
             dealt = placed.tile([P, PASSES, PACK, P], I32, name=name, align_bytes=64, offset=offset)
-            nc.scalar.copy(
-                dealt[:].bitcast(U32).rearrange("p a t m -> p a t m"),
-                raw[:].bitcast(U32).rearrange("p a (m t) -> p a t m", t=PACK),
+            engine_copy(
+                dealt[:].bitcast(view).rearrange("p a t m -> p a m t"),
+                raw[:].bitcast(view).rearrange("p a (m t) -> p a m t", t=PACK),
             )
             return dealt
 
@@ -75,7 +75,6 @@ def tile_list_xcross_noneP_kernel(
         nc.sync.dma_start(weight_scales[ROW0:P:SPREAD, 0, :].bitcast(I32), dn_scales.rearrange("a q n -> q a n").bitcast(I32))
         nc.sync.dma_start(weight_scales[ROW0:P:SPREAD, 1, :].bitcast(I32), wb_scales.rearrange("a q n -> q a n").bitcast(I32))
         nc.sync.dma_start(scale_window[ROW0:P:SPREAD, :].bitcast(I32), tab_scales.rearrange("a q c -> q a c").bitcast(I32))
-        wb_raw = load_words(wb_words, "wb_raw", 81920)
         planes = keep.tile([P, PASSES, J + 2 * N], U8, name="planes", align_bytes=64)
         nc.vector.memset(planes[:].bitcast(I32), 0)
 
@@ -85,7 +84,7 @@ def tile_list_xcross_noneP_kernel(
         nc.sync.dma_start(word_window[:], tab_words[0].rearrange("p t i -> p (t i)").bitcast(I32))
         up_raw = placed.tile([P, PACK, N], F32, name="up_raw", offset=36864)
         nc.sync.dma_start(up_raw[:], upw.rearrange("(p i) n -> p i n", i=PACK))
-        dn_codes = deal_words(dn_raw, "dn_codes", 86016)
+        dn_codes = deal_words(dn_raw, "dn_codes", 86016, nc.scalar.copy, U32)
 
         scale_rows = keep.tile([P, J + 2 * N], U8, name="scale_rows")
         nc.vector.tensor_copy(
@@ -100,7 +99,8 @@ def tile_list_xcross_noneP_kernel(
                 planes[32 * quad : 32 * quad + 4].bitcast(I32),
                 scale_rows[ROW0 + 8 * SPREAD * quad : ROW0 + 8 * SPREAD * (quad + 1) : SPREAD, :].bitcast(I32),
             )
-        wb_codes = deal_words(wb_raw, "wb_codes", 98304)
+        wb_raw = load_words(wb_words, "wb_raw", 61440 - 4096)
+        wb_codes = deal_words(wb_raw, "wb_codes", 98304, nc.vector.tensor_copy, I32)
         x0 = [load_x0(0, 61440)]
 
         up_rounded = placed.tile([P, N * PACK], BF16, name="up_rounded", align_bytes=64, offset=0)

@@ -60,13 +60,13 @@ def tile_list_xcross_noneP_kernel(
             nc.sync.dma_start(window[:], x0_rows[:, t, :])
             return window
 
+
+        bias = placed.tile([P, PACK], F32, name="bias", offset=102400)
+        nc.sync.dma_start(bias[:, 0:PACK], b.rearrange("(p t) -> p t", t=PACK))
+
+        dn_raw = load_words(dn_words, "dn_raw", 77824)
         offsets = keep.tile([P, J // 16], U16, name="offsets")
         nc.sync.dma_start(offsets[:], offs)
-
-        bias = keep.tile([P, PACK], F32, name="bias")
-        nc.sync.dma_start(bias[:, 0:PACK], b.rearrange("(p t) -> p t", t=PACK))
-        dn_raw = load_words(dn_words, "dn_raw", 77824)
-
         scale_window = placed.tile([P, T], U8, name="scale_window", offset=98304)
         weight_scales = keep.tile([P, 2, N], U8, name="weight_scales")
         nc.vector.memset(weight_scales[:].bitcast(I32), 0)
@@ -75,11 +75,11 @@ def tile_list_xcross_noneP_kernel(
         nc.sync.dma_start(weight_scales[ROW0:P:SPREAD, 0, :].bitcast(I32), dn_scales.rearrange("a q n -> q a n").bitcast(I32))
         nc.sync.dma_start(weight_scales[ROW0:P:SPREAD, 1, :].bitcast(I32), wb_scales.rearrange("a q n -> q a n").bitcast(I32))
         nc.sync.dma_start(scale_window[ROW0:P:SPREAD, :].bitcast(I32), tab_scales.rearrange("a q c -> q a c").bitcast(I32))
-        planes = keep.tile([P, PASSES, J + 2 * N], U8, name="planes", align_bytes=64)
-        nc.vector.memset(planes[:].bitcast(I32), 0)
 
         bias_one = keep.tile([P, PACK], F32, name="bias_one")
         nc.vector.tensor_scalar_add(bias_one[:], bias[:, 0:PACK], 1.0)
+        planes = placed.tile([P, PASSES, J + 2 * N], U8, name="planes", align_bytes=64, offset=102400)
+        nc.vector.memset(planes[:].bitcast(I32), 0)
         word_window = placed.tile([P, T], I32, name="word_window", offset=20480)
         nc.sync.dma_start(word_window[:], tab_words[0].rearrange("p t i -> p (t i)").bitcast(I32))
         up_raw = placed.tile([P, PACK, N], F32, name="up_raw", offset=36864)
@@ -116,7 +116,7 @@ def tile_list_xcross_noneP_kernel(
         def first_stage(half):
             rounded = placed.tile([P, HALF, PACK], BF16, name="h_rounded%d" % half, align_bytes=64, offset=(8192, 94208)[half])
             for c0 in range(0, HALF, CHUNK):
-                for t0, empty in ((0, nc.scalar.copy), (2, nc.vector.tensor_copy if half else nc.scalar.copy)):
+                for t0 in (0, 2):
                     bank = psum.tile([P, 2, CHUNK], F32, name="h_bank", tag="bank")
                     for t in range(t0, t0 + 2):
                         for a in range(PASSES):
@@ -129,6 +129,7 @@ def tile_list_xcross_noneP_kernel(
                                 start=(a == 0),
                                 stop=(a == PASSES - 1),
                             )
+                    empty = nc.vector.tensor_copy if (half, c0, t0) == (1, CHUNK, 0) else nc.scalar.copy
                     empty(rounded[:, c0 : c0 + CHUNK, t0 : t0 + 2], bank[:].rearrange("p t j -> p j t"))
             codes = keep.tile([P, HALF], I32, name="h_codes%d" % half, align_bytes=64)
             scales = keep.tile([P, HALF], U8, name="h_scales%d" % half, align_bytes=64)

@@ -61,14 +61,11 @@ def tile_list_xcross_noneP_kernel(
             return window
 
 
-        bias = placed.tile([P, PACK], F32, name="bias", offset=102400)
-        nc.sync.dma_start(bias[:, 0:PACK], b.rearrange("(p t) -> p t", t=PACK))
-
         dn_raw = load_words(dn_words, "dn_raw", 77824)
-        offsets = keep.tile([P, J // 16], U16, name="offsets")
+        offsets = keep.tile([P, J // 16], U16, name="offsets", align_bytes=256)
         nc.sync.dma_start(offsets[:], offs)
         scale_window = placed.tile([P, T], U8, name="scale_window", offset=98304)
-        weight_scales = keep.tile([P, 2, N], U8, name="weight_scales")
+        weight_scales = keep.tile([P, 2, N], U8, name="weight_scales", align_bytes=256)
         nc.vector.memset(weight_scales[:].bitcast(I32), 0)
         nc.vector.memset(scale_window[:, 0 : T // 2].bitcast(I32), 0)
         nc.gpsimd.memset(scale_window[:, T // 2 :].bitcast(I32), 0)
@@ -76,17 +73,13 @@ def tile_list_xcross_noneP_kernel(
         nc.sync.dma_start(weight_scales[ROW0:P:SPREAD, 1, :].bitcast(I32), wb_scales.rearrange("a q n -> q a n").bitcast(I32))
         nc.sync.dma_start(scale_window[ROW0:P:SPREAD, :].bitcast(I32), tab_scales.rearrange("a q c -> q a c").bitcast(I32))
 
-        bias_one = keep.tile([P, PACK], F32, name="bias_one")
-        nc.vector.tensor_scalar_add(bias_one[:], bias[:, 0:PACK], 1.0)
-        planes = placed.tile([P, PASSES, J + 2 * N], U8, name="planes", align_bytes=64, offset=102400)
-        nc.vector.memset(planes[:].bitcast(I32), 0)
         word_window = placed.tile([P, T], I32, name="word_window", offset=20480)
         nc.sync.dma_start(word_window[:], tab_words[0].rearrange("p t i -> p (t i)").bitcast(I32))
         up_raw = placed.tile([P, PACK, N], F32, name="up_raw", offset=36864)
         nc.sync.dma_start(up_raw[:], upw.rearrange("(p i) n -> p i n", i=PACK))
         dn_codes = deal_words(dn_raw, "dn_codes", 86016, nc.scalar.copy, U32)
 
-        scale_rows = keep.tile([P, J + 2 * N], U8, name="scale_rows")
+        scale_rows = keep.tile([P, J + 2 * N], U8, name="scale_rows", align_bytes=256)
         nc.vector.tensor_copy(
             scale_rows[:, J:].rearrange("p (w t m) -> p w t m", w=2, t=PACK),
             weight_scales[:].rearrange("p w (m t) -> p w t m", t=PACK),
@@ -94,13 +87,18 @@ def tile_list_xcross_noneP_kernel(
         picked_scales = placed.tile([P, J], U8, name="picked_scales", offset=61440 - 512)
         nc.vector.tensor_copy(picked_scales[:], scale_window[:].indirect(offsets[:]))
         nc.vector.tensor_copy(scale_rows[:, 0:J].bitcast(I32), picked_scales[:].bitcast(I32))
+        planes = placed.tile([P, PASSES, J + 2 * N], U8, name="planes", align_bytes=256, offset=77824)
         for quad in (0, 2, 1, 3):
             nc.sync.dma_start(
                 planes[32 * quad : 32 * quad + 4].bitcast(I32),
                 scale_rows[ROW0 + 8 * SPREAD * quad : ROW0 + 8 * SPREAD * (quad + 1) : SPREAD, :].bitcast(I32),
             )
         wb_raw = load_words(wb_words, "wb_raw", 61440 - 4096)
-        wb_codes = deal_words(wb_raw, "wb_codes", 98304, nc.vector.tensor_copy, I32)
+        bias = placed.tile([P, PACK], F32, name="bias", offset=98304)
+        nc.sync.dma_start(bias[:], b.rearrange("(p t) -> p t", t=PACK))
+        bias_one = keep.tile([P, PACK], F32, name="bias_one")
+        nc.vector.tensor_scalar_add(bias_one[:], bias[:], 1.0)
+        wb_codes = deal_words(wb_raw, "wb_codes", 102400, nc.vector.tensor_copy, I32)
         x0 = [load_x0(0, 61440)]
 
         up_rounded = placed.tile([P, N * PACK], BF16, name="up_rounded", align_bytes=64, offset=0)
@@ -171,7 +169,7 @@ def tile_list_xcross_noneP_kernel(
             return bank
 
         out_rows = out_0.rearrange("(p t) j -> p t j", t=PACK)
-        crossed = keep.tile([P, PACK, J], F32, name="crossed")
+        crossed = keep.tile([P, PACK, J], F32, name="crossed", align_bytes=256)
         low = crossed[:, 0:2, :]
         high = crossed[:, 2:4, :]
         starts = [sum(PIECES[:i]) for i in range(len(PIECES))]
@@ -221,8 +219,8 @@ def tile_list_xcross_noneP_kernel(
             if half == 0:
                 store_rows(0, 2 * J + HALF)
 
-        out_codes = keep.tile([P, J], I32, name="out_codes", align_bytes=64)
-        out_scales = keep.tile([P, J], U8, name="out_scales", align_bytes=64)
+        out_codes = keep.tile([P, J], I32, name="out_codes", align_bytes=256)
+        out_scales = keep.tile([P, J], U8, name="out_scales", align_bytes=256)
         code_rows = out_1[0].rearrange("p j i -> p (j i)").bitcast(I32)
         pieces = [slice(starts[i], starts[i] + PIECES[i]) for i in range(len(PIECES))]
 
@@ -257,10 +255,11 @@ def tile_list_xcross_noneP_kernel(
         quantise(1)
         store_codes(0, HALF)
         quantise(2)
+        store_codes(HALF, starts[3])
         quantise(3)
-        store_codes(HALF, J)
+        store_codes(starts[3], J)
         for quad in range(4):
-            queue = nc.scalar if quad % 2 else nc.sync
+            queue = nc.scalar if quad else nc.sync
             queue.dma_start(
                 out_2[0, 4 * quad : 4 * quad + 4, :].bitcast(I32), out_scales[32 * quad : 32 * quad + 4, :].bitcast(I32)
             )

@@ -20,8 +20,7 @@ IDENTITY = mybir.ActivationFunctionType.Identity
 P = 128
 PACK = 4
 PASSES = K // (P * PACK)
-SPREAD = 3
-ROW0 = 32
+SPREAD = 4
 HALF = 512
 CHUNK = 256
 PIECES = (256, 256, 256, 256)
@@ -69,9 +68,9 @@ def tile_list_xcross_noneP_kernel(
         nc.vector.memset(weight_scales[:].bitcast(I32), 0)
         nc.vector.memset(scale_window[:, 0 : T // 2].bitcast(I32), 0)
         nc.gpsimd.memset(scale_window[:, T // 2 :].bitcast(I32), 0)
-        nc.sync.dma_start(weight_scales[ROW0:P:SPREAD, 0, :].bitcast(I32), dn_scales.rearrange("a q n -> q a n").bitcast(I32))
-        nc.sync.dma_start(weight_scales[ROW0:P:SPREAD, 1, :].bitcast(I32), wb_scales.rearrange("a q n -> q a n").bitcast(I32))
-        nc.sync.dma_start(scale_window[ROW0:P:SPREAD, :].bitcast(I32), tab_scales.rearrange("a q c -> q a c").bitcast(I32))
+        nc.sync.dma_start(weight_scales[0:P:SPREAD, 0, :].bitcast(I32), dn_scales.rearrange("a q n -> (a q) n").bitcast(I32))
+        nc.sync.dma_start(weight_scales[0:P:SPREAD, 1, :].bitcast(I32), wb_scales.rearrange("a q n -> (a q) n").bitcast(I32))
+        nc.sync.dma_start(scale_window[0:P:SPREAD, :].bitcast(I32), tab_scales.rearrange("a q c -> (a q) c").bitcast(I32))
 
         word_window = placed.tile([P, T], I32, name="word_window", offset=20480)
         nc.sync.dma_start(word_window[:], tab_words[0].rearrange("p t i -> p (t i)").bitcast(I32))
@@ -79,19 +78,21 @@ def tile_list_xcross_noneP_kernel(
         nc.sync.dma_start(up_raw[:], upw.rearrange("(p i) n -> p i n", i=PACK))
         dn_codes = deal_words(dn_raw, "dn_codes", 86016, nc.scalar.copy, U32)
 
-        scale_rows = keep.tile([P, J + 2 * N], U8, name="scale_rows", align_bytes=256)
+        scale_rows = keep.tile([P, PASSES, J + 2 * N], U8, name="scale_rows", align_bytes=256)
         nc.vector.tensor_copy(
-            scale_rows[:, J:].rearrange("p (w t m) -> p w t m", w=2, t=PACK),
+            scale_rows[:, 0, J:].rearrange("p (w t m) -> p w t m", w=2, t=PACK),
             weight_scales[:].rearrange("p w (m t) -> p w t m", t=PACK),
         )
+        nc.vector.tensor_copy(scale_rows[0:64, 1, J:].bitcast(I32), scale_rows[64:P, 0, J:].bitcast(I32))
         picked_scales = placed.tile([P, J], U8, name="picked_scales", offset=61440 - 512)
         nc.vector.tensor_copy(picked_scales[:], scale_window[:].indirect(offsets[:]))
-        nc.vector.tensor_copy(scale_rows[:, 0:J].bitcast(I32), picked_scales[:].bitcast(I32))
+        for a in range(PASSES):
+            nc.vector.tensor_copy(scale_rows[0:64, a, 0:J].bitcast(I32), picked_scales[64 * a : 64 * (a + 1), :].bitcast(I32))
         planes = placed.tile([P, PASSES, J + 2 * N], U8, name="planes", align_bytes=256, offset=77824)
-        for quad in (0, 2, 1, 3):
+        for r in range(4):
             nc.sync.dma_start(
-                planes[32 * quad : 32 * quad + 4].bitcast(I32),
-                scale_rows[ROW0 + 8 * SPREAD * quad : ROW0 + 8 * SPREAD * (quad + 1) : SPREAD, :].bitcast(I32),
+                planes[r:P:32].rearrange("p a c -> p (a c)").bitcast(I32),
+                scale_rows[SPREAD * r : 64 : 4 * SPREAD].rearrange("p a c -> p (a c)").bitcast(I32),
             )
         wb_raw = load_words(wb_words, "wb_raw", 61440 - 4096)
         bias = placed.tile([P, PACK], F32, name="bias", offset=98304)

@@ -60,6 +60,10 @@ def tile_list_xcross_noneP_kernel(
             return window
 
 
+        bias = keep.tile([P, PACK], F32, name="bias")
+        nc.sync.dma_start(bias[:], b.rearrange("(p t) -> p t", t=PACK))
+        bias_one = keep.tile([P, PACK], F32, name="bias_one")
+        nc.scalar.add(bias_one[:], bias[:], 1.0)
         dn_raw = load_words(dn_words, "dn_raw", 77824)
         offsets = keep.tile([P, J // 16], U16, name="offsets", align_bytes=256)
         nc.sync.dma_start(offsets[:], offs)
@@ -95,10 +99,6 @@ def tile_list_xcross_noneP_kernel(
                 scale_rows[SPREAD * r : 64 : 4 * SPREAD].rearrange("p a c -> p (a c)").bitcast(I32),
             )
         wb_raw = load_words(wb_words, "wb_raw", 61440 - 4096)
-        bias = placed.tile([P, PACK], F32, name="bias", offset=98304)
-        nc.sync.dma_start(bias[:], b.rearrange("(p t) -> p t", t=PACK))
-        bias_one = keep.tile([P, PACK], F32, name="bias_one")
-        nc.vector.tensor_scalar_add(bias_one[:], bias[:], 1.0)
         wb_codes = deal_words(wb_raw, "wb_codes", 102400, nc.vector.tensor_copy, I32)
         x0 = [load_x0(0, 61440)]
 
@@ -256,11 +256,10 @@ def tile_list_xcross_noneP_kernel(
         quantise(1)
         store_codes(0, HALF)
         quantise(2)
-        store_codes(HALF, starts[3])
         quantise(3)
-        store_codes(starts[3], J)
+        store_codes(HALF, J)
         for quad in range(4):
-            queue = nc.scalar if quad else nc.sync
+            queue = nc.scalar if quad % 2 else nc.sync
             queue.dma_start(
                 out_2[0, 4 * quad : 4 * quad + 4, :].bitcast(I32), out_scales[32 * quad : 32 * quad + 4, :].bitcast(I32)
             )

@@ -60,10 +60,6 @@ def tile_list_xcross_noneP_kernel(
             return window
 
 
-        bias = keep.tile([P, PACK], F32, name="bias")
-        nc.sync.dma_start(bias[:], b.rearrange("(p t) -> p t", t=PACK))
-        bias_one = keep.tile([P, PACK], F32, name="bias_one")
-        nc.scalar.add(bias_one[:], bias[:], 1.0)
         dn_raw = load_words(dn_words, "dn_raw", 77824)
         offsets = keep.tile([P, J // 16], U16, name="offsets", align_bytes=256)
         nc.sync.dma_start(offsets[:], offs)
@@ -99,6 +95,10 @@ def tile_list_xcross_noneP_kernel(
                 scale_rows[SPREAD * r : 64 : 4 * SPREAD].rearrange("p a c -> p (a c)").bitcast(I32),
             )
         wb_raw = load_words(wb_words, "wb_raw", 61440 - 4096)
+        bias = placed.tile([P, PACK], F32, name="bias", offset=98304)
+        nc.sync.dma_start(bias[:], b.rearrange("(p t) -> p t", t=PACK))
+        bias_one = keep.tile([P, PACK], F32, name="bias_one")
+        nc.scalar.add(bias_one[:], bias[:], 1.0)
         wb_codes = deal_words(wb_raw, "wb_codes", 102400, nc.vector.tensor_copy, I32)
         x0 = [load_x0(0, 61440)]
 

from contextlib import ExitStack

import concourse.mybir as mybir

K, R, N, T, J = 1024, 512, 512, 4096, 1024
FLOPS = 2 * J * (K * R + K * N + R * N)

F32 = mybir.dt.float32
BF16 = mybir.dt.bfloat16
I32 = mybir.dt.int32
U32 = mybir.dt.uint32
U16 = mybir.dt.uint16
U8 = mybir.dt.uint8
FP8X4 = mybir.dt.float8_e4m3fn_x4
FP4X4 = mybir.dt.float4_e2m1fn_x4
MULT = mybir.AluOpType.mult
ADD = mybir.AluOpType.add
IDENTITY = mybir.ActivationFunctionType.Identity

P = 128
PACK = 4
PASSES = K // (P * PACK)
SPREAD = 4
HALF = 512
CHUNK = 256
PIECES = (256, 256, 256, 256)


def tile_list_xcross_noneP_kernel(
    tc, tab_words, tab_scales, wb_words, wb_scales, dn_words, dn_scales, upw, x0T, b, offs, out_0, out_1, out_2
):
    nc = tc.nc
    with ExitStack() as ctx:
        keep = ctx.enter_context(tc.tile_pool(name="keep", bufs=1))
        placed = ctx.enter_context(tc.tile_pool(name="placed", bufs=1))
        psum = ctx.enter_context(tc.psum_pool(name="psum", bufs=4))


        def entries(j0, width):
            return offsets[:, j0 // 16 : (j0 + width) // 16]

        def load_words(words, name, offset):
            raw = placed.tile([P, PASSES, N], I32, name=name, offset=offset)
            nc.sync.dma_start(raw[:], words.rearrange("a p n i -> p a (n i)").bitcast(I32))
            return raw

        def deal_words(raw, name, offset, engine_copy, view):
            dealt = placed.tile([P, PASSES, PACK, P], I32, name=name, align_bytes=64, offset=offset)
            engine_copy(
                dealt[:].bitcast(view).rearrange("p a t m -> p a m t"),
                raw[:].bitcast(view).rearrange("p a (m t) -> p a m t", t=PACK),
            )
            return dealt

        x0_rows = x0T.rearrange("(p t) c -> p t c", t=PACK)

        def load_x0(t, offset):
            window = placed.tile([P, T], F32, name="x0_%d" % t, offset=offset)
            nc.sync.dma_start(window[:], x0_rows[:, t, :])
            return window


        dn_raw = load_words(dn_words, "dn_raw", 77824)
        offsets = keep.tile([P, J // 16], U16, name="offsets", align_bytes=256)
        nc.sync.dma_start(offsets[:], offs)
        scale_window = placed.tile([P, T], U8, name="scale_window", offset=98304)
        weight_scales = keep.tile([P, 2, N], U8, name="weight_scales", align_bytes=256)
        nc.vector.memset(weight_scales[:].bitcast(I32), 0)
        nc.vector.memset(scale_window[:, 0 : T // 2].bitcast(I32), 0)
        nc.gpsimd.memset(scale_window[:, T // 2 :].bitcast(I32), 0)
        nc.sync.dma_start(weight_scales[0:P:SPREAD, 0, :].bitcast(I32), dn_scales.rearrange("a q n -> (a q) n").bitcast(I32))
        nc.sync.dma_start(weight_scales[0:P:SPREAD, 1, :].bitcast(I32), wb_scales.rearrange("a q n -> (a q) n").bitcast(I32))
        nc.sync.dma_start(scale_window[0:P:SPREAD, :].bitcast(I32), tab_scales.rearrange("a q c -> (a q) c").bitcast(I32))

        word_window = placed.tile([P, T], I32, name="word_window", offset=20480)
        nc.sync.dma_start(word_window[:], tab_words[0].rearrange("p t i -> p (t i)").bitcast(I32))
        up_raw = placed.tile([P, PACK, N], F32, name="up_raw", offset=36864)
        nc.sync.dma_start(up_raw[:], upw.rearrange("(p i) n -> p i n", i=PACK))
        dn_codes = deal_words(dn_raw, "dn_codes", 86016, nc.scalar.copy, U32)

        scale_rows = keep.tile([P, PASSES, J + 2 * N], U8, name="scale_rows", align_bytes=256)
        nc.vector.tensor_copy(
            scale_rows[:, 0, J:].rearrange("p (w t m) -> p w t m", w=2, t=PACK),
            weight_scales[:].rearrange("p w (m t) -> p w t m", t=PACK),
        )
        nc.vector.tensor_copy(scale_rows[0:64, 1, J:].bitcast(I32), scale_rows[64:P, 0, J:].bitcast(I32))
        picked_scales = placed.tile([P, J], U8, name="picked_scales", offset=61440 - 512)
        nc.vector.tensor_copy(picked_scales[:], scale_window[:].indirect(offsets[:]))
        for a in range(PASSES):
            nc.vector.tensor_copy(scale_rows[0:64, a, 0:J].bitcast(I32), picked_scales[64 * a : 64 * (a + 1), :].bitcast(I32))
        planes = placed.tile([P, PASSES, J + 2 * N], U8, name="planes", align_bytes=256, offset=77824)
        for r in range(4):
            nc.sync.dma_start(
                planes[r:P:32].rearrange("p a c -> p (a c)").bitcast(I32),
                scale_rows[SPREAD * r : 64 : 4 * SPREAD].rearrange("p a c -> p (a c)").bitcast(I32),
            )
        wb_raw = load_words(wb_words, "wb_raw", 61440 - 4096)
        bias = placed.tile([P, PACK], F32, name="bias", offset=98304)
        nc.sync.dma_start(bias[:], b.rearrange("(p t) -> p t", t=PACK))
        bias_one = keep.tile([P, PACK], F32, name="bias_one")
        nc.scalar.add(bias_one[:], bias[:], 1.0)
        wb_codes = deal_words(wb_raw, "wb_codes", 102400, nc.vector.tensor_copy, I32)
        x0 = [load_x0(0, 61440)]

        up_rounded = placed.tile([P, N * PACK], BF16, name="up_rounded", align_bytes=64, offset=0)
        up_dealt = up_rounded[:].rearrange("p (t m i) -> p m t i", t=PACK, i=PACK)

        def gather_words(half):
            picked = placed.tile([P, HALF], U32, name="picked%d" % half, offset=(4096 - 1024, 2048)[half])
            nc.vector.tensor_copy(picked[:], word_window[:].bitcast(U32).indirect(entries(half * HALF, HALF)))
            parted = keep.tile([P, PASSES, HALF], U16, name="parted%d" % half, align_bytes=64)
            nc.vector.tensor_copy(parted[:], picked[:].bitcast(U16).rearrange("p (j a) -> p a j", a=PASSES))
            return parted

        def first_stage(half):
            rounded = placed.tile([P, HALF, PACK], BF16, name="h_rounded%d" % half, align_bytes=64, offset=(8192, 94208)[half])
            for c0 in range(0, HALF, CHUNK):
                for t0 in (0, 2):
                    bank = psum.tile([P, 2, CHUNK], F32, name="h_bank", tag="bank")
                    for t in range(t0, t0 + 2):
                        for a in range(PASSES):
                            nc.tensor.matmul_mx(
                                out=bank[:, t - t0, :],
                                lhsT=dn_codes[:, a, t, :].bitcast(FP8X4),
                                lhsT_scale=planes[:, a, J + t * P : J + (t + 1) * P],
                                rhs=v_codes[half][:, a, c0 : c0 + CHUNK].bitcast(FP4X4),
                                rhs_scale=planes[:, a, half * HALF + c0 : half * HALF + c0 + CHUNK],
                                start=(a == 0),
                                stop=(a == PASSES - 1),
                            )
                    empty = nc.vector.tensor_copy if (half, c0, t0) == (1, CHUNK, 0) else nc.scalar.copy
                    empty(rounded[:, c0 : c0 + CHUNK, t0 : t0 + 2], bank[:].rearrange("p t j -> p j t"))
            codes = keep.tile([P, HALF], I32, name="h_codes%d" % half, align_bytes=64)
            scales = keep.tile([P, HALF], U8, name="h_scales%d" % half, align_bytes=64)
            nc.vector.quantize_mx(
                out=codes[:].bitcast(FP8X4), scales=scales[:], in_=rounded[:].rearrange("p j t -> p (j t)")
            )
            return codes, scales

        v_codes = [gather_words(0)]
        v_codes.append(gather_words(1))
        x0.append(load_x0(1, 20480))
        nc.vector.tensor_copy(up_dealt, up_raw[:].rearrange("p i (m t) -> p m t i", t=PACK))
        up_codes = keep.tile([P, N], I32, name="up_codes", align_bytes=64)
        up_planes = keep.tile([P, N], U8, name="up_planes", align_bytes=64)
        nc.vector.quantize_mx(out=up_codes[:].bitcast(FP8X4), scales=up_planes[:], in_=up_rounded[:])

        def second_stage(t, half):
            h_codes, h_scales = h[half]
            bank = psum.tile([P, HALF], F32, name="y_bank", tag="bank")
            for a in range(PASSES):
                nc.tensor.matmul_mx(
                    out=bank[:],
                    lhsT=wb_codes[:, a, t, :].bitcast(FP8X4),
                    lhsT_scale=planes[:, a, J + N + t * P : J + N + (t + 1) * P],
                    rhs=v_codes[half][:, a, :].bitcast(FP4X4),
                    rhs_scale=planes[:, a, half * HALF : (half + 1) * HALF],
                    start=(a == 0),
                    stop=False,
                )
            nc.tensor.matmul_mx(
                out=bank[:],
                lhsT=up_codes[:, t * P : (t + 1) * P].bitcast(FP8X4),
                lhsT_scale=up_planes[:, t * P : (t + 1) * P],
                rhs=h_codes[:].bitcast(FP8X4),
                rhs_scale=h_scales[:],
                start=False,
                stop=True,
            )
            return bank

        out_rows = out_0.rearrange("(p t) j -> p t j", t=PACK)
        crossed = keep.tile([P, PACK, J], F32, name="crossed", align_bytes=256)
        low = crossed[:, 0:2, :]
        high = crossed[:, 2:4, :]
        starts = [sum(PIECES[:i]) for i in range(len(PIECES))]
        rounded = [
            keep.tile([P, width, PACK], BF16, name="out_rounded%d" % i, align_bytes=64)
            for i, width in enumerate(PIECES)
        ]

        h = [first_stage(0)]
        x0.append(load_x0(2, 4096))
        h.append(first_stage(1))
        y = {(t, half): second_stage(t, half) for t, half in ((0, 0), (1, 0), (0, 1), (1, 1))}

        halves = [slice(0, HALF), slice(HALF, J)]

        first = placed.tile([P, HALF], F32, name="first_factor", offset=45056)

        def make_factor(t):
            made = keep.tile([P, J], F32, name="factor%d" % t)
            parts = [first[:] if (t, half) == (0, 0) else made[:, halves[half]] for half in range(2)]
            for half in range(2):
                bank = y[t, half] if (t, half) in y else second_stage(t, half)
                nc.scalar.activation(parts[half], bank[:], IDENTITY, bias=bias_one[:, t : t + 1])
            return made

        factors = [make_factor(t) for t in range(PACK)]
        factor = factors[3]
        for half in range(2):
            for t in range(2):
                made = first[:] if (t, half) == (0, 0) else factors[t][:, halves[half]]
                nc.vector.tensor_tensor(crossed[:, t, halves[half]], x0[t][:].indirect(entries(half * HALF, HALF)), made, MULT)
        x0.append(load_x0(3, 36864))
        for i in range(len(PIECES)):
            nc.scalar.copy(
                rounded[i][:, :, 0:2], low[:, :, starts[i] : starts[i] + PIECES[i]].rearrange("p t j -> p j t")
            )
        flat_rows = out_0.rearrange("(p t) j -> p (t j)", t=PACK)
        flat = crossed[:].rearrange("p t j -> p (t j)")

        def store_rows(c0, c1):
            nc.sync.dma_start(flat_rows[:, c0:c1], flat[:, c0:c1])

        for half in range(2):
            nc.vector.tensor_tensor(
                high[:, 0, halves[half]], x0[2][:].indirect(entries(half * HALF, HALF)), factors[2][:, halves[half]], MULT
            )
            if half == 0:
                store_rows(0, 2 * J + HALF)

        out_codes = keep.tile([P, J], I32, name="out_codes", align_bytes=256)
        out_scales = keep.tile([P, J], U8, name="out_scales", align_bytes=256)
        code_rows = out_1[0].rearrange("p j i -> p (j i)").bitcast(I32)
        pieces = [slice(starts[i], starts[i] + PIECES[i]) for i in range(len(PIECES))]

        def cross(i):
            nc.vector.tensor_tensor(
                high[:, 1, pieces[i]], x0[3][:].indirect(entries(starts[i], PIECES[i])), factor[:, pieces[i]], MULT
            )

        def round_high(i, engine_copy):
            engine_copy(rounded[i][:, :, 2:4], high[:, :, pieces[i]].rearrange("p t j -> p j t"))

        def quantise(i):
            nc.vector.quantize_mx(
                out=out_codes[:, pieces[i]].bitcast(FP8X4),
                scales=out_scales[:, pieces[i]],
                in_=rounded[i][:].rearrange("p j t -> p (j t)"),
            )

        def store_codes(c0, c1):
            nc.sync.dma_start(code_rows[:, c0:c1], out_codes[:, c0:c1])

        cross(0)
        cross(1)
        store_rows(2 * J + HALF, 3 * J + HALF)
        cross(3)
        cross(2)
        store_rows(3 * J + HALF, 4 * J)
        for i in (0, 1, 3):
            round_high(i, nc.scalar.copy)
        quantise(0)
        round_high(2, nc.vector.tensor_copy)
        quantise(1)
        store_codes(0, HALF)
        quantise(2)
        quantise(3)
        store_codes(HALF, J)
        for quad in range(4):
            queue = nc.scalar if quad % 2 else nc.sync
            queue.dma_start(
                out_2[0, 4 * quad : 4 * quad + 4, :].bitcast(I32), out_scales[32 * quad : 32 * quad + 4, :].bitcast(I32)
            )
